import numpy as np
import ml_dtypes


def mxq(x, axis, fmt="e4m3"):
    dtype, down = {"e4m3": (ml_dtypes.float8_e4m3fn, 7), "e5m2": (ml_dtypes.float8_e5m2, 14)}[fmt]
    v = np.moveaxis(np.asarray(x, np.float32).astype(ml_dtypes.bfloat16).astype(np.float64), axis, -1)
    blocks = v.reshape(v.shape[:-1] + (-1, 32))
    amax = np.abs(blocks).max(-1, keepdims=True)
    byte = np.maximum(np.where(amax > 0, np.frexp(amax)[1] - 1 + 127, 0) - down, 1)
    scale = np.exp2(byte - 127.0)
    codes = (blocks / scale).astype(np.float32).astype(dtype).astype(np.float64)
    return np.moveaxis((codes * scale).reshape(v.shape), -1, axis)


WIDE = False


def mx_kscale(k):
    if not WIDE:
        return np.ones(k)
    levels = np.array([10, -10, 5, -5, 0])
    if k % 512:
        return np.exp2(np.random.permutation(np.resize(levels, k // 32))).repeat(32)
    a = np.empty((k // 512, 16))
    for p in range(k // 512):
        a[p, :8] = np.random.permutation(np.resize(levels, 8))
        for g in range(8):
            far = levels[np.abs(levels - a[p, g]) >= 10]
            a[p, g + 8] = far[np.random.randint(len(far))]
    return np.exp2(a.ravel()).repeat(32)


def f64(x):
    return np.asarray(x).astype(np.float64)


def striped(idx):
    return np.tile(idx.reshape(-1, 16).T, (8, 1)).astype(np.uint16)


def unstriped(offs):
    return offs[:16].T.reshape(-1).astype(np.int64)


def pack_weight(w):
    k, n = w.shape
    w = f64(np.asarray(w, np.float32).astype(ml_dtypes.bfloat16)).reshape(k // 32, 32, n)
    amax = np.abs(w).max(1)
    byte = np.clip(np.where(amax > 0, np.frexp(amax)[1] - 1 + 127 - 7, 1), 1, 254)
    scaled = (w * np.exp2(127.0 - byte)[:, None, :]).reshape(k, n).astype(np.float32)
    words = np.ascontiguousarray(scaled.reshape(k // 512, 128, 4, n).transpose(0, 1, 3, 2)).astype(ml_dtypes.float8_e4m3fn).view(np.uint8)
    return words, np.ascontiguousarray(byte.astype(np.uint8).reshape(k // 512, 16, n))


def unpack_weight(words, scales):
    g, p, n, _ = words.shape
    vals = np.ascontiguousarray(words).view(ml_dtypes.float8_e4m3fn).astype(np.float64) * np.repeat(np.exp2(scales.astype(np.float64) - 127.0), 8, axis=1)[..., None]
    return vals.transpose(0, 1, 3, 2).reshape(g * 512, n)


def relu(v):
    return np.maximum(v, 0.0)


K, T, S, H, N, U = 1024, 2048, 1024, 512, 256, 2048
P = 2 ** 7


def setup_inputs():
    n = np.random.standard_normal
    s = mx_kscale(K)[:, None]
    u = mx_kscale(H)
    packed_xT = pack_weight(n((K, T)) * s)
    return {
        "x_words": packed_xT[0],
        "x_scales": packed_xT[1],
        "gate": np.tile(np.random.uniform(0.5, 1.5, S), (P, 1)).astype(np.float32),
        "w1": (n((K, H)) / np.sqrt(K) / s * u).astype(np.float32),
        "w2": (n((H, N)) / np.sqrt(H) / u[:, None]).astype(np.float32),
        "offs": striped(np.random.permutation(T)[:S]),
        "dst": striped(np.random.permutation(U)[:S]),
    }


def reference(x_words, x_scales, gate, w1, w2, offs, dst):
    xq = unpack_weight(x_words, x_scales)[:, unstriped(offs)]
    h = relu(mxq(f64(w1), 0, "e4m3").T @ xq)
    y = mxq(f64(w2), 0, "e4m3").T @ mxq(h, 0, "e4m3")
    out = np.zeros((N, U))
    out[:, unstriped(dst)] = y * f64(gate)[:1]
    return out

@@ -1,0 +1,194 @@
+from contextlib import ExitStack
+
+import concourse.mybir as mybir
+
+K, T, S, H, N, U = 1024, 2048, 1024, 512, 256, 2048
+FLOPS = 2 * S * (K * H + H * N)
+
+F32 = mybir.dt.float32
+BF16 = mybir.dt.bfloat16
+I32 = mybir.dt.int32
+U32 = mybir.dt.uint32
+U16 = mybir.dt.uint16
+U8 = mybir.dt.uint8
+FP8X4 = mybir.dt.float8_e4m3fn_x4
+RELU = mybir.ActivationFunctionType.Relu
+MULT = mybir.AluOpType.mult
+
+P = 128
+PACK = 4
+K_PASS = P * PACK
+PASSES = K // K_PASS
+STRIPE = 16
+BLOCK = 128
+CHUNKS = ((0, 256), (256, 512), (512, 1024))
+
+
+def tile_picked_route2_mlprelu_p_kernel(tc, x_words, x_scales, gate, w1, w2, offs, dst, out):
+    nc = tc.nc
+    with ExitStack() as ctx:
+        sb = ctx.enter_context(tc.tile_pool(name="sb", bufs=1))
+        psum = ctx.enter_context(tc.psum_pool(name="psum", bufs=1))
+
+        def tile(name, width, dtype):
+            return sb.tile([P, width], dtype, name=name, align_bytes=64)
+
+        def entries(list_tile, lo, hi):
+            return list_tile[:, lo // STRIPE : hi // STRIPE]
+
+        offs_sb = tile("offs_sb", S // STRIPE, U16)
+        dst_sb = tile("dst_sb", S // STRIPE, U16)
+        x_planes = tile("x_planes", T, U8)
+        x_table = [tile("x_table%d" % z, T, U32) for z in range(PASSES)]
+        placed = [tile("placed%d" % m, U, F32) for m in range(N // P)]
+        gate_sb = tile("gate_sb", S, F32)
+        half = H // 2
+        w1_raw = [[tile("w1_raw%d_%d" % (z, u), PACK * half, F32) for u in range(2)] for z in range(PASSES)]
+        w2_raw = [tile("w2_raw%d" % m, PACK * P, F32) for m in range(N // P)]
+
+        def load_words(z):
+            nc.sync.dma_start(
+                out=x_table[z][:].bitcast(I32),
+                in_=x_words[z].rearrange("p c r -> p (c r)").bitcast(I32),
+            )
+
+        def load_w2(m):
+            nc.sync.dma_start(
+                out=w2_raw[m][:].rearrange("p (j c) -> p j c", j=PACK),
+                in_=w2[:, m * P : (m + 1) * P].rearrange("(p j) c -> p j c", j=PACK),
+            )
+
+        nc.vector.memset(x_planes[:].bitcast(I32), 0)
+        nc.sync.dma_start(offs_sb[:], offs)
+        load_words(0)
+        for q in range(4):
+            nc.sync.dma_start(
+                out=x_planes[32 * q : 32 * q + 4 * PASSES, :].bitcast(I32),
+                in_=x_scales[:, 4 * q : 4 * q + 4, :].bitcast(I32),
+            )
+        for z in range(PASSES):
+            for u in range(2):
+                nc.sync.dma_start(
+                    out=w1_raw[z][u][:].rearrange("p (j c) -> p j c", j=PACK),
+                    in_=w1[z * K_PASS : (z + 1) * K_PASS, u * half : (u + 1) * half].rearrange("(p j) c -> p j c", j=PACK),
+                )
+        load_words(1)
+        load_w2(0)
+        nc.sync.dma_start(dst_sb[:], dst)
+        first = CHUNKS[0][1]
+        nc.sync.dma_start(out=gate_sb[:, :first], in_=gate[:, :first])
+        load_w2(1)
+        nc.sync.dma_start(out=gate_sb[:, first:], in_=gate[:, first:])
+        for m in range(N // P):
+            nc.vector.memset(placed[m][:], 0.0)
+
+        words0 = tile("words0", S, U32)
+        nc.vector.tensor_copy(words0[:], x_table[0][:].indirect(offs_sb[:]))
+        planes = tile("planes", S, U8)
+        nc.vector.tensor_copy(planes[:], x_planes[:].indirect(offs_sb[:]))
+
+        w1_codes, w1_scales = [], []
+        for z in range(PASSES):
+            grouped = tile("w1_grouped%d" % z, PACK * H, BF16)
+            view = grouped[:].rearrange("p (t m j) -> p m t j", t=PACK, j=PACK)
+            for u in range(2):
+                src = w1_raw[z][u][:].rearrange("p (j m t) -> p m t j", j=PACK, t=PACK)
+                dst_view = view[:, u * (P // 2) : (u + 1) * (P // 2)]
+                if z == PASSES - 1 and u == 1:
+                    nc.vector.tensor_copy(out=dst_view, in_=src)
+                else:
+                    nc.scalar.copy(out=dst_view, in_=src)
+            codes = tile("w1_codes%d" % z, H, U32)
+            scales = tile("w1_scales%d" % z, H, U8)
+            nc.vector.quantize_mx(out=codes[:].bitcast(FP8X4), scales=scales[:], in_=grouped[:])
+            w1_codes.append(codes)
+            w1_scales.append(scales)
+
+        words1 = []
+        for c, (lo, hi) in enumerate(CHUNKS):
+            words = tile("words1_%d" % c, hi - lo, U32)
+            nc.vector.tensor_copy(words[:], x_table[1][:].indirect(entries(offs_sb, lo, hi)))
+            words1.append(words)
+
+        w2_codes, w2_scales = [], []
+
+        def prepare_w2(m):
+            grouped = tile("w2_grouped%d" % m, PACK * P, BF16)
+            nc.scalar.copy(
+                out=grouped[:].rearrange("p (c i j) -> p c j i", i=4, j=PACK),
+                in_=w2_raw[m][:].rearrange("p (j c i) -> p c j i", i=4, j=PACK),
+            )
+            codes = tile("w2_codes%d" % m, P, U32)
+            scales = tile("w2_scales%d" % m, P, U8)
+            nc.vector.quantize_mx(out=codes[:].bitcast(FP8X4), scales=scales[:], in_=grouped[:])
+            w2_codes.append(codes)
+            w2_scales.append(scales)
+
+        h_codes, h_scales = [], []
+
+        def hidden(c):
+            lo, hi = CHUNKS[c]
+            grouped = tile("h_grouped%d" % c, PACK * (hi - lo), BF16)
+            for b0 in range(lo, hi, BLOCK):
+                bank = psum.tile([P, PACK * BLOCK], F32, name="bank%d" % (b0 // BLOCK))
+                for t in range(PACK):
+                    cols = slice(t * P, (t + 1) * P)
+                    for z in range(PASSES):
+                        moving = words0[:, b0 : b0 + BLOCK] if z == 0 else words1[c][:, b0 - lo : b0 - lo + BLOCK]
+                        nc.tensor.matmul_mx(
+                            out=bank[:, t * BLOCK : (t + 1) * BLOCK],
+                            lhsT=w1_codes[z][:, cols].bitcast(FP8X4),
+                            lhsT_scale=w1_scales[z][:, cols],
+                            rhs=moving.bitcast(FP8X4),
+                            rhs_scale=planes[4 * z :, b0 : b0 + BLOCK],
+                            start=(z == 0),
+                            stop=(z == PASSES - 1),
+                        )
+                nc.scalar.activation(
+                    out=grouped[:, PACK * (b0 - lo) : PACK * (b0 - lo + BLOCK)].rearrange("p (n t) -> p n t", t=PACK),
+                    in_=bank[:].rearrange("p (t n) -> p n t", t=PACK),
+                    func=RELU,
+                )
+            codes = tile("h_codes%d" % c, hi - lo, U32)
+            scales = tile("h_scales%d" % c, hi - lo, U8)
+            nc.vector.quantize_mx(out=codes[:].bitcast(FP8X4), scales=scales[:], in_=grouped[:])
+            h_codes.append(codes)
+            h_scales.append(scales)
+
+        y = [tile("y%d" % m, S, F32) for m in range(N // P)]
+
+        def product(m, c, bank_number):
+            lo, hi = CHUNKS[c]
+            bank = psum.tile([P, PACK * BLOCK], F32, name="bank%d" % bank_number)
+            nc.tensor.matmul_mx(
+                out=bank[:, : hi - lo],
+                lhsT=w2_codes[m][:].bitcast(FP8X4),
+                lhsT_scale=w2_scales[m][:],
+                rhs=h_codes[c][:].bitcast(FP8X4),
+                rhs_scale=h_scales[c][:],
+                start=True,
+                stop=True,
+            )
+            nc.scalar.copy(out=y[m][:, lo:hi], in_=bank[:, : hi - lo])
+
+        def place(m, lo, hi):
+            nc.vector.tensor_tensor(placed[m][:].indirect(entries(dst_sb, lo, hi)), y[m][:, lo:hi], gate_sb[:, lo:hi], MULT)
+
+        prepare_w2(0)
+        hidden(0)
+        product(0, 0, 0)
+        place(0, *CHUNKS[0])
+        prepare_w2(1)
+        hidden(1)
+        product(1, 0, 3)
+        place(1, *CHUNKS[0])
+        hidden(2)
+        product(0, 1, 7)
+        place(0, *CHUNKS[1])
+        product(0, 2, 1)
+        place(0, *CHUNKS[2])
+        nc.sync.dma_start(out=out[:P, :], in_=placed[0][:])
+        product(1, 1, 2)
+        product(1, 2, 4)
+        place(1, CHUNKS[1][0], S)
+        nc.sync.dma_start(out=out[P:, :], in_=placed[1][:])

@@ -28,23 +28,27 @@ def tile_picked_route2_mlprelu_p_kernel(tc, x_words, x_scales, gate, w1, w2, off
     nc = tc.nc
     with ExitStack() as ctx:
         sb = ctx.enter_context(tc.tile_pool(name="sb", bufs=1))
+        reused = ctx.enter_context(tc.tile_pool(name="reused", bufs=1))
         psum = ctx.enter_context(tc.psum_pool(name="psum", bufs=1))
 
         def tile(name, width, dtype):
             return sb.tile([P, width], dtype, name=name, align_bytes=64)
+
+        def tile_at(name, width, dtype, offset):
+            return reused.tile([P, width], dtype, name=name, align_bytes=64, offset=offset)
 
         def entries(list_tile, lo, hi):
             return list_tile[:, lo // STRIPE : hi // STRIPE]
 
         offs_sb = tile("offs_sb", S // STRIPE, U16)
         dst_sb = tile("dst_sb", S // STRIPE, U16)
-        x_planes = tile("x_planes", T, U8)
-        x_table = [tile("x_table%d" % z, T, U32) for z in range(PASSES)]
+        x_planes = tile_at("x_planes", T, U8, 0)
+        x_table = [tile("x_table0", T, U32), tile_at("x_table1", T, U32, 8192)]
         placed = [tile("placed%d" % m, U, F32) for m in range(N // P)]
         gate_sb = tile("gate_sb", S, F32)
-        half = H // 2
-        w1_raw = [[tile("w1_raw%d_%d" % (z, u), PACK * half, F32) for u in range(2)] for z in range(PASSES)]
-        w2_raw = [tile("w2_raw%d" % m, PACK * P, F32) for m in range(N // P)]
+        w1_raw = [tile("w1_raw%d" % z, PACK * H, F32) for z in range(PASSES)]
+        w2_raw = tile("w2_raw", PACK * N, F32)
+        zero = tile("zero", 1, F32)
 
         def load_words(z):
             nc.sync.dma_start(
@@ -52,35 +56,32 @@ def tile_picked_route2_mlprelu_p_kernel(tc, x_words, x_scales, gate, w1, w2, off
                 in_=x_words[z].rearrange("p c r -> p (c r)").bitcast(I32),
             )
 
-        def load_w2(m):
-            nc.sync.dma_start(
-                out=w2_raw[m][:].rearrange("p (j c) -> p j c", j=PACK),
-                in_=w2[:, m * P : (m + 1) * P].rearrange("(p j) c -> p j c", j=PACK),
-            )
-
         nc.vector.memset(x_planes[:].bitcast(I32), 0)
-        nc.sync.dma_start(offs_sb[:], offs)
-        load_words(0)
+        nc.vector.memset(zero[:], 0.0)
         for q in range(4):
-            nc.sync.dma_start(
+            nc.gpsimd.dma_start(
                 out=x_planes[32 * q : 32 * q + 4 * PASSES, :].bitcast(I32),
                 in_=x_scales[:, 4 * q : 4 * q + 4, :].bitcast(I32),
             )
+        load_words(0)
+        nc.sync.dma_start(offs_sb[:], offs)
         for z in range(PASSES):
-            for u in range(2):
-                nc.sync.dma_start(
-                    out=w1_raw[z][u][:].rearrange("p (j c) -> p j c", j=PACK),
-                    in_=w1[z * K_PASS : (z + 1) * K_PASS, u * half : (u + 1) * half].rearrange("(p j) c -> p j c", j=PACK),
-                )
+            nc.sync.dma_start(
+                out=w1_raw[z][:].rearrange("p (j c) -> p j c", j=PACK),
+                in_=w1[z * K_PASS : (z + 1) * K_PASS, :].rearrange("(p j) c -> p j c", j=PACK),
+            )
         load_words(1)
-        load_w2(0)
+        for t in range(PACK):
+            nc.sync.dma_start(
+                out=w2_raw[:, t * N : (t + 1) * N],
+                in_=w2.rearrange("(g t r) c -> t g r c", t=PACK, r=8)[t],
+            )
         nc.sync.dma_start(dst_sb[:], dst)
         first = CHUNKS[0][1]
         nc.sync.dma_start(out=gate_sb[:, :first], in_=gate[:, :first])
-        load_w2(1)
         nc.sync.dma_start(out=gate_sb[:, first:], in_=gate[:, first:])
         for m in range(N // P):
-            nc.vector.memset(placed[m][:], 0.0)
+            nc.scalar.copy(out=placed[m][:], in_=zero[:].to_broadcast([P, U]))
 
         words0 = tile("words0", S, U32)
         nc.vector.tensor_copy(words0[:], x_table[0][:].indirect(offs_sb[:]))
@@ -89,40 +90,34 @@ def tile_picked_route2_mlprelu_p_kernel(tc, x_words, x_scales, gate, w1, w2, off
 
         w1_codes, w1_scales = [], []
         for z in range(PASSES):
-            grouped = tile("w1_grouped%d" % z, PACK * H, BF16)
-            view = grouped[:].rearrange("p (t m j) -> p m t j", t=PACK, j=PACK)
-            for u in range(2):
-                src = w1_raw[z][u][:].rearrange("p (j m t) -> p m t j", j=PACK, t=PACK)
-                dst_view = view[:, u * (P // 2) : (u + 1) * (P // 2)]
-                if z == PASSES - 1 and u == 1:
+            grouped = tile("w1_grouped0", PACK * H, BF16) if z == 0 else tile_at("w1_grouped1", PACK * H, BF16, 1024)
+            for t in range(PACK):
+                src = w1_raw[z][:].rearrange("p (j g t h i) -> p t g h j i", j=PACK, t=PACK, h=2, i=4)[:, t]
+                dst_view = grouped[:, t * K_PASS : (t + 1) * K_PASS].rearrange("p (g h i j) -> p g h j i", h=2, i=4, j=PACK)
+                if z == PASSES - 1 and t < 2:
                     nc.vector.tensor_copy(out=dst_view, in_=src)
                 else:
                     nc.scalar.copy(out=dst_view, in_=src)
             codes = tile("w1_codes%d" % z, H, U32)
-            scales = tile("w1_scales%d" % z, H, U8)
+            scales = tile_at("w1_scales0", H, U8, 0) if z == 0 else tile("w1_scales1", H, U8)
             nc.vector.quantize_mx(out=codes[:].bitcast(FP8X4), scales=scales[:], in_=grouped[:])
             w1_codes.append(codes)
             w1_scales.append(scales)
 
         words1 = []
         for c, (lo, hi) in enumerate(CHUNKS):
-            words = tile("words1_%d" % c, hi - lo, U32)
+            words = tile_at("words1_%d" % c, hi - lo, U32, 1024 + 4 * lo)
             nc.vector.tensor_copy(words[:], x_table[1][:].indirect(entries(offs_sb, lo, hi)))
             words1.append(words)
 
-        w2_codes, w2_scales = [], []
-
-        def prepare_w2(m):
-            grouped = tile("w2_grouped%d" % m, PACK * P, BF16)
-            nc.scalar.copy(
-                out=grouped[:].rearrange("p (c i j) -> p c j i", i=4, j=PACK),
-                in_=w2_raw[m][:].rearrange("p (j c i) -> p c j i", i=4, j=PACK),
-            )
-            codes = tile("w2_codes%d" % m, P, U32)
-            scales = tile("w2_scales%d" % m, P, U8)
-            nc.vector.quantize_mx(out=codes[:].bitcast(FP8X4), scales=scales[:], in_=grouped[:])
-            w2_codes.append(codes)
-            w2_scales.append(scales)
+        w2_grouped = tile_at("w2_grouped", PACK * N, BF16, 8192)
+        nc.vector.tensor_copy(
+            out=w2_grouped[:].rearrange("p (c i j) -> p c j i", i=4, j=PACK),
+            in_=w2_raw[:].rearrange("p (j c i) -> p c j i", i=4, j=PACK),
+        )
+        w2_codes = tile("w2_codes", N, U32)
+        w2_scales = tile("w2_scales", N, U8)
+        nc.vector.quantize_mx(out=w2_codes[:].bitcast(FP8X4), scales=w2_scales[:], in_=w2_grouped[:])
 
         h_codes, h_scales = [], []
 
@@ -162,8 +157,8 @@ def tile_picked_route2_mlprelu_p_kernel(tc, x_words, x_scales, gate, w1, w2, off
             bank = psum.tile([P, PACK * BLOCK], F32, name="bank%d" % bank_number)
             nc.tensor.matmul_mx(
                 out=bank[:, : hi - lo],
-                lhsT=w2_codes[m][:].bitcast(FP8X4),
-                lhsT_scale=w2_scales[m][:],
+                lhsT=w2_codes[:, m * P : (m + 1) * P].bitcast(FP8X4),
+                lhsT_scale=w2_scales[:, m * P : (m + 1) * P],
                 rhs=h_codes[c][:].bitcast(FP8X4),
                 rhs_scale=h_scales[c][:],
                 start=True,
@@ -174,11 +169,9 @@ def tile_picked_route2_mlprelu_p_kernel(tc, x_words, x_scales, gate, w1, w2, off
         def place(m, lo, hi):
             nc.vector.tensor_tensor(placed[m][:].indirect(entries(dst_sb, lo, hi)), y[m][:, lo:hi], gate_sb[:, lo:hi], MULT)
 
-        prepare_w2(0)
         hidden(0)
         product(0, 0, 0)
         place(0, *CHUNKS[0])
-        prepare_w2(1)
         hidden(1)
         product(1, 0, 3)
         place(1, *CHUNKS[0])

@@ -48,7 +48,6 @@ def tile_picked_route2_mlprelu_p_kernel(tc, x_words, x_scales, gate, w1, w2, off
         gate_sb = tile("gate_sb", S, F32)
         w1_raw = [tile("w1_raw%d" % z, PACK * H, F32) for z in range(PASSES)]
         w2_raw = tile("w2_raw", PACK * N, F32)
-        zero = tile("zero", 1, F32)
 
         def load_words(z):
             nc.sync.dma_start(
@@ -57,14 +56,13 @@ def tile_picked_route2_mlprelu_p_kernel(tc, x_words, x_scales, gate, w1, w2, off
             )
 
         nc.vector.memset(x_planes[:].bitcast(I32), 0)
-        nc.vector.memset(zero[:], 0.0)
+        load_words(0)
+        nc.sync.dma_start(offs_sb[:], offs)
         for q in range(4):
-            nc.gpsimd.dma_start(
+            nc.sync.dma_start(
                 out=x_planes[32 * q : 32 * q + 4 * PASSES, :].bitcast(I32),
                 in_=x_scales[:, 4 * q : 4 * q + 4, :].bitcast(I32),
             )
-        load_words(0)
-        nc.sync.dma_start(offs_sb[:], offs)
         for z in range(PASSES):
             nc.sync.dma_start(
                 out=w1_raw[z][:].rearrange("p (j c) -> p j c", j=PACK),
@@ -80,8 +78,8 @@ def tile_picked_route2_mlprelu_p_kernel(tc, x_words, x_scales, gate, w1, w2, off
         first = CHUNKS[0][1]
         nc.sync.dma_start(out=gate_sb[:, :first], in_=gate[:, :first])
         nc.sync.dma_start(out=gate_sb[:, first:], in_=gate[:, first:])
-        for m in range(N // P):
-            nc.scalar.copy(out=placed[m][:], in_=zero[:].to_broadcast([P, U]))
+        nc.vector.memset(placed[0][:], 0.0)
+        nc.gpsimd.memset(placed[1][:], 0.0)
 
         words0 = tile("words0", S, U32)
         nc.vector.tensor_copy(words0[:], x_table[0][:].indirect(offs_sb[:]))

@@ -21,6 +21,7 @@ K_PASS = P * PACK
 PASSES = K // K_PASS
 STRIPE = 16
 BLOCK = 128
+AHEAD = 512
 CHUNKS = ((0, 256), (256, 512), (512, 1024))
 
 
@@ -43,11 +44,11 @@ def tile_picked_route2_mlprelu_p_kernel(tc, x_words, x_scales, gate, w1, w2, off
         offs_sb = tile("offs_sb", S // STRIPE, U16)
         dst_sb = tile("dst_sb", S // STRIPE, U16)
         x_planes = tile_at("x_planes", T, U8, 0)
-        x_table = [tile("x_table0", T, U32), tile_at("x_table1", T, U32, 8192)]
+        x_table = [tile("x_table0", T, U32), tile("x_table1", T, U32)]
         placed = [tile("placed%d" % m, U, F32) for m in range(N // P)]
         gate_sb = tile("gate_sb", S, F32)
         w1_raw = [tile("w1_raw%d" % z, PACK * H, F32) for z in range(PASSES)]
-        w2_raw = tile("w2_raw", PACK * N, F32)
+        w2_raw = tile_at("w2_raw", PACK * N, F32, 8192)
 
         def load_words(z):
             nc.sync.dma_start(
@@ -102,51 +103,65 @@ def tile_picked_route2_mlprelu_p_kernel(tc, x_words, x_scales, gate, w1, w2, off
             w1_codes.append(codes)
             w1_scales.append(scales)
 
-        words1 = []
-        for c, (lo, hi) in enumerate(CHUNKS):
-            words = tile_at("words1_%d" % c, hi - lo, U32, 1024 + 4 * lo)
-            nc.vector.tensor_copy(words[:], x_table[1][:].indirect(entries(offs_sb, lo, hi)))
-            words1.append(words)
+        banks = {}
 
-        w2_grouped = tile_at("w2_grouped", PACK * N, BF16, 8192)
-        nc.vector.tensor_copy(
-            out=w2_grouped[:].rearrange("p (c i j) -> p c j i", i=4, j=PACK),
-            in_=w2_raw[:].rearrange("p (j c i) -> p c j i", i=4, j=PACK),
-        )
-        w2_codes = tile("w2_codes", N, U32)
-        w2_scales = tile("w2_scales", N, U8)
-        nc.vector.quantize_mx(out=w2_codes[:].bitcast(FP8X4), scales=w2_scales[:], in_=w2_grouped[:])
+        def first_product(z, b0, moving, opens):
+            if opens:
+                banks[b0] = psum.tile([P, PACK * BLOCK], F32, name="bank%d" % (b0 // BLOCK))
+            for t in range(PACK):
+                cols = slice(t * P, (t + 1) * P)
+                nc.tensor.matmul_mx(
+                    out=banks[b0][:, t * BLOCK : (t + 1) * BLOCK],
+                    lhsT=w1_codes[z][:, cols].bitcast(FP8X4),
+                    lhsT_scale=w1_scales[z][:, cols],
+                    rhs=moving.bitcast(FP8X4),
+                    rhs_scale=planes[4 * z :, b0 : b0 + BLOCK],
+                    start=(opens and t == 0),
+                    stop=(not opens and t == PACK - 1),
+                )
+
+        for b0 in range(0, AHEAD, BLOCK):
+            first_product(0, b0, words0[:, b0 : b0 + BLOCK], True)
+
+        def second_pass(lo, words):
+            for at in range(0, words.shape[1], BLOCK):
+                b0 = lo + at
+                first_product(1, b0, words[:, at : at + BLOCK], b0 >= AHEAD)
+                if b0 >= AHEAD:
+                    first_product(0, b0, words0[:, b0 : b0 + BLOCK], False)
+
+        def gather_words1(lo, hi, offset):
+            words = tile_at("words1_%d" % lo, hi - lo, U32, offset)
+            nc.vector.tensor_copy(words[:], x_table[1][:].indirect(entries(offs_sb, lo, hi)))
+            return words[:]
 
         h_codes, h_scales = [], []
 
-        def hidden(c):
+        def hidden(c, grouped):
             lo, hi = CHUNKS[c]
-            grouped = tile("h_grouped%d" % c, PACK * (hi - lo), BF16)
             for b0 in range(lo, hi, BLOCK):
-                bank = psum.tile([P, PACK * BLOCK], F32, name="bank%d" % (b0 // BLOCK))
-                for t in range(PACK):
-                    cols = slice(t * P, (t + 1) * P)
-                    for z in range(PASSES):
-                        moving = words0[:, b0 : b0 + BLOCK] if z == 0 else words1[c][:, b0 - lo : b0 - lo + BLOCK]
-                        nc.tensor.matmul_mx(
-                            out=bank[:, t * BLOCK : (t + 1) * BLOCK],
-                            lhsT=w1_codes[z][:, cols].bitcast(FP8X4),
-                            lhsT_scale=w1_scales[z][:, cols],
-                            rhs=moving.bitcast(FP8X4),
-                            rhs_scale=planes[4 * z :, b0 : b0 + BLOCK],
-                            start=(z == 0),
-                            stop=(z == PASSES - 1),
-                        )
                 nc.scalar.activation(
                     out=grouped[:, PACK * (b0 - lo) : PACK * (b0 - lo + BLOCK)].rearrange("p (n t) -> p n t", t=PACK),
-                    in_=bank[:].rearrange("p (t n) -> p n t", t=PACK),
+                    in_=banks[b0][:].rearrange("p (t n) -> p n t", t=PACK),
                     func=RELU,
                 )
-            codes = tile("h_codes%d" % c, hi - lo, U32)
+            codes = tile_at("h_codes%d" % c, hi - lo, U32, 8192 + 4 * lo) if c < 2 else tile("h_codes%d" % c, hi - lo, U32)
             scales = tile("h_scales%d" % c, hi - lo, U8)
             nc.vector.quantize_mx(out=codes[:].bitcast(FP8X4), scales=scales[:], in_=grouped[:])
             h_codes.append(codes)
             h_scales.append(scales)
+
+        second_pass(0, gather_words1(0, 256, 2048))
+        second_pass(256, gather_words1(256, 768, 3072))
+        w2_grouped = tile_at("w2_grouped", PACK * N, BF16, 1024)
+        nc.vector.tensor_copy(
+            out=w2_grouped[:].rearrange("p (c i j) -> p c j i", i=4, j=PACK),
+            in_=w2_raw[:].rearrange("p (j c i) -> p c j i", i=4, j=PACK),
+        )
+        hidden(0, tile_at("h_grouped0", 1024, BF16, 12288))
+        w2_codes = tile("w2_codes", N, U32)
+        w2_scales = tile("w2_scales", N, U8)
+        nc.vector.quantize_mx(out=w2_codes[:].bitcast(FP8X4), scales=w2_scales[:], in_=w2_grouped[:])
 
         y = [tile("y%d" % m, S, F32) for m in range(N // P)]
 
@@ -167,19 +182,20 @@ def tile_picked_route2_mlprelu_p_kernel(tc, x_words, x_scales, gate, w1, w2, off
         def place(m, lo, hi):
             nc.vector.tensor_tensor(placed[m][:].indirect(entries(dst_sb, lo, hi)), y[m][:, lo:hi], gate_sb[:, lo:hi], MULT)
 
-        hidden(0)
-        product(0, 0, 0)
+        product(0, 0, 6)
+        product(1, 0, 7)
+        second_pass(768, gather_words1(768, S, 12288))
         place(0, *CHUNKS[0])
-        hidden(1)
-        product(1, 0, 3)
+        hidden(1, tile("h_grouped1", 1024, BF16))
         place(1, *CHUNKS[0])
-        hidden(2)
-        product(0, 1, 7)
+        product(0, 1, 2)
         place(0, *CHUNKS[1])
-        product(0, 2, 1)
+        hidden(2, tile_at("h_grouped2", 2048, BF16, 5120))
+        product(1, 1, 7)
+        place(1, *CHUNKS[1])
+        product(0, 2, 4)
+        product(1, 2, 5)
         place(0, *CHUNKS[2])
         nc.sync.dma_start(out=out[:P, :], in_=placed[0][:])
-        product(1, 1, 2)
-        product(1, 2, 4)
-        place(1, CHUNKS[1][0], S)
+        place(1, *CHUNKS[2])
         nc.sync.dma_start(out=out[P:, :], in_=placed[1][:])

@@ -47,8 +47,8 @@ def tile_picked_route2_mlprelu_p_kernel(tc, x_words, x_scales, gate, w1, w2, off
         x_table = [tile("x_table0", T, U32), tile("x_table1", T, U32)]
         placed = [tile("placed%d" % m, U, F32) for m in range(N // P)]
         gate_sb = tile("gate_sb", S, F32)
-        w1_raw = [tile("w1_raw%d" % z, PACK * H, F32) for z in range(PASSES)]
-        w2_raw = tile_at("w2_raw", PACK * N, F32, 8192)
+        w1_raw = [tile("w1_raw0", PACK * H, F32), tile_at("w1_raw1", PACK * H, F32, 16384)]
+        w2_raw = [tile_at("w2_raw%d" % u, 2 * N, F32, 8192 + 2048 * u) for u in range(2)]
 
         def load_words(z):
             nc.sync.dma_start(
@@ -72,7 +72,7 @@ def tile_picked_route2_mlprelu_p_kernel(tc, x_words, x_scales, gate, w1, w2, off
         load_words(1)
         for t in range(PACK):
             nc.sync.dma_start(
-                out=w2_raw[:, t * N : (t + 1) * N],
+                out=w2_raw[t // 2][:, (t % 2) * N : (t % 2 + 1) * N],
                 in_=w2.rearrange("(g t r) c -> t g r c", t=PACK, r=8)[t],
             )
         nc.sync.dma_start(dst_sb[:], dst)
@@ -98,7 +98,7 @@ def tile_picked_route2_mlprelu_p_kernel(tc, x_words, x_scales, gate, w1, w2, off
                 else:
                     nc.scalar.copy(out=dst_view, in_=src)
             codes = tile("w1_codes%d" % z, H, U32)
-            scales = tile_at("w1_scales0", H, U8, 0) if z == 0 else tile("w1_scales1", H, U8)
+            scales = tile("w1_scales%d" % z, H, U8)
             nc.vector.quantize_mx(out=codes[:].bitcast(FP8X4), scales=scales[:], in_=grouped[:])
             w1_codes.append(codes)
             w1_scales.append(scales)
@@ -145,20 +145,21 @@ def tile_picked_route2_mlprelu_p_kernel(tc, x_words, x_scales, gate, w1, w2, off
                     in_=banks[b0][:].rearrange("p (t n) -> p n t", t=PACK),
                     func=RELU,
                 )
-            codes = tile_at("h_codes%d" % c, hi - lo, U32, 8192 + 4 * lo) if c < 2 else tile("h_codes%d" % c, hi - lo, U32)
+            codes = tile_at("h_codes%d" % c, hi - lo, U32, 11264 - 4 * lo) if c < 2 else tile("h_codes%d" % c, hi - lo, U32)
             scales = tile("h_scales%d" % c, hi - lo, U8)
             nc.vector.quantize_mx(out=codes[:].bitcast(FP8X4), scales=scales[:], in_=grouped[:])
             h_codes.append(codes)
             h_scales.append(scales)
 
-        second_pass(0, gather_words1(0, 256, 2048))
-        second_pass(256, gather_words1(256, 768, 3072))
-        w2_grouped = tile_at("w2_grouped", PACK * N, BF16, 1024)
-        nc.vector.tensor_copy(
-            out=w2_grouped[:].rearrange("p (c i j) -> p c j i", i=4, j=PACK),
-            in_=w2_raw[:].rearrange("p (j c i) -> p c j i", i=4, j=PACK),
-        )
-        hidden(0, tile_at("h_grouped0", 1024, BF16, 12288))
+        second_pass(0, gather_words1(0, 256, 16384))
+        second_pass(256, gather_words1(256, 768, 17408))
+        w2_grouped = tile("w2_grouped", PACK * N, BF16)
+        for u, engine_copy in enumerate((nc.scalar.copy, nc.vector.tensor_copy)):
+            engine_copy(
+                out=w2_grouped[:].rearrange("p (c i u e) -> p u c e i", i=4, u=2, e=2)[:, u],
+                in_=w2_raw[u][:].rearrange("p (e c i) -> p c e i", i=4, e=2),
+            )
+        hidden(0, tile_at("h_grouped0", 1024, BF16, 8192))
         w2_codes = tile("w2_codes", N, U32)
         w2_scales = tile("w2_scales", N, U8)
         nc.vector.quantize_mx(out=w2_codes[:].bitcast(FP8X4), scales=w2_scales[:], in_=w2_grouped[:])
@@ -184,13 +185,13 @@ def tile_picked_route2_mlprelu_p_kernel(tc, x_words, x_scales, gate, w1, w2, off
 
         product(0, 0, 6)
         product(1, 0, 7)
-        second_pass(768, gather_words1(768, S, 12288))
+        second_pass(768, gather_words1(768, S, 8192))
         place(0, *CHUNKS[0])
         hidden(1, tile("h_grouped1", 1024, BF16))
         place(1, *CHUNKS[0])
         product(0, 1, 2)
         place(0, *CHUNKS[1])
-        hidden(2, tile_at("h_grouped2", 2048, BF16, 5120))
+        hidden(2, tile_at("h_grouped2", 2048, BF16, 11264))
         product(1, 1, 7)
         place(1, *CHUNKS[1])
         product(0, 2, 4)

@@ -87,21 +87,28 @@ def tile_picked_route2_mlprelu_p_kernel(tc, x_words, x_scales, gate, w1, w2, off
         planes = tile("planes", S, U8)
         nc.vector.tensor_copy(planes[:], x_planes[:].indirect(offs_sb[:]))
 
-        w1_codes, w1_scales = [], []
-        for z in range(PASSES):
-            grouped = tile("w1_grouped0", PACK * H, BF16) if z == 0 else tile_at("w1_grouped1", PACK * H, BF16, 1024)
-            for t in range(PACK):
-                src = w1_raw[z][:].rearrange("p (j g t h i) -> p t g h j i", j=PACK, t=PACK, h=2, i=4)[:, t]
-                dst_view = grouped[:, t * K_PASS : (t + 1) * K_PASS].rearrange("p (g h i j) -> p g h j i", h=2, i=4, j=PACK)
-                if z == PASSES - 1 and t < 2:
-                    nc.vector.tensor_copy(out=dst_view, in_=src)
-                else:
-                    nc.scalar.copy(out=dst_view, in_=src)
-            codes = tile("w1_codes%d" % z, H, U32)
-            scales = tile("w1_scales%d" % z, H, U8)
-            nc.vector.quantize_mx(out=codes[:].bitcast(FP8X4), scales=scales[:], in_=grouped[:])
-            w1_codes.append(codes)
-            w1_scales.append(scales)
+        w1_codes = [tile("w1_codes%d" % z, H, U32) for z in range(PASSES)]
+        w1_scales = [tile("w1_scales%d" % z, H, U8) for z in range(PASSES)]
+
+        def round_w1(engine_copy, z, t, grouped, at):
+            engine_copy(
+                out=grouped[:, at * K_PASS : (at + 1) * K_PASS].rearrange("p (g h i j) -> p g h j i", h=2, i=4, j=PACK),
+                in_=w1_raw[z][:].rearrange("p (j g t h i) -> p t g h j i", j=PACK, t=PACK, h=2, i=4)[:, t],
+            )
+
+        def quantise_w1(z, t0, t1, grouped):
+            cols = slice(t0 * P, t1 * P)
+            nc.vector.quantize_mx(out=w1_codes[z][:, cols].bitcast(FP8X4), scales=w1_scales[z][:, cols], in_=grouped[:])
+
+        grouped0 = tile_at("w1_grouped0", PACK * H, BF16, 2048)
+        for t in range(PACK):
+            round_w1(nc.scalar.copy, 0, t, grouped0, t)
+        quantise_w1(0, 0, PACK, grouped0)
+        halves = [tile_at("w1_grouped1_0", 2 * K_PASS, BF16, 1024), tile("w1_grouped1_1", 2 * K_PASS, BF16)]
+        for t in range(PACK):
+            round_w1(nc.vector.tensor_copy if t < 2 else nc.scalar.copy, 1, t, halves[t // 2], t % 2)
+        for u in (1, 0):
+            quantise_w1(1, 2 * u, 2 * u + 2, halves[u])
 
         banks = {}
 
@@ -159,10 +166,10 @@ def tile_picked_route2_mlprelu_p_kernel(tc, x_words, x_scales, gate, w1, w2, off
                 out=w2_grouped[:].rearrange("p (c i u e) -> p u c e i", i=4, u=2, e=2)[:, u],
                 in_=w2_raw[u][:].rearrange("p (e c i) -> p c e i", i=4, e=2),
             )
-        hidden(0, tile_at("h_grouped0", 1024, BF16, 8192))
         w2_codes = tile("w2_codes", N, U32)
         w2_scales = tile("w2_scales", N, U8)
         nc.vector.quantize_mx(out=w2_codes[:].bitcast(FP8X4), scales=w2_scales[:], in_=w2_grouped[:])
+        hidden(0, tile_at("h_grouped0", 1024, BF16, 8192))
 
         y = [tile("y%d" % m, S, F32) for m in range(N // P)]
 

@@ -22,6 +22,8 @@ PASSES = K // K_PASS
 STRIPE = 16
 BLOCK = 128
 AHEAD = 512
+BLOCK_BANK = (0, 1, 2, 3, 4, 3, 4, 3)
+FIRST = 256
 CHUNKS = ((0, 256), (256, 512), (512, 1024))
 
 
@@ -43,12 +45,11 @@ def tile_picked_route2_mlprelu_p_kernel(tc, x_words, x_scales, gate, w1, w2, off
 
         offs_sb = tile("offs_sb", S // STRIPE, U16)
         dst_sb = tile("dst_sb", S // STRIPE, U16)
-        x_planes = tile_at("x_planes", T, U8, 0)
-        x_table = [tile("x_table0", T, U32), tile("x_table1", T, U32)]
+        x_rows = tile_at("x_rows", T, U8, 0)
+        x_table = [tile_at("x_table0", T, U32, 8192)]
         placed = [tile("placed%d" % m, U, F32) for m in range(N // P)]
-        gate_sb = tile("gate_sb", S, F32)
-        w1_raw = [tile("w1_raw0", PACK * H, F32), tile_at("w1_raw1", PACK * H, F32, 16384)]
-        w2_raw = [tile_at("w2_raw%d" % u, 2 * N, F32, 8192 + 2048 * u) for u in range(2)]
+        planes = tile("planes", PASSES * S, U8)
+        zero = tile("zero", 16, F32)
 
         def load_words(z):
             nc.sync.dma_start(
@@ -56,132 +57,145 @@ def tile_picked_route2_mlprelu_p_kernel(tc, x_words, x_scales, gate, w1, w2, off
                 in_=x_words[z].rearrange("p c r -> p (c r)").bitcast(I32),
             )
 
-        nc.vector.memset(x_planes[:].bitcast(I32), 0)
-        load_words(0)
-        nc.sync.dma_start(offs_sb[:], offs)
-        for q in range(4):
+        def load_w1(z, raw):
             nc.sync.dma_start(
-                out=x_planes[32 * q : 32 * q + 4 * PASSES, :].bitcast(I32),
-                in_=x_scales[:, 4 * q : 4 * q + 4, :].bitcast(I32),
-            )
-        for z in range(PASSES):
-            nc.sync.dma_start(
-                out=w1_raw[z][:].rearrange("p (j c) -> p j c", j=PACK),
+                out=raw[:].rearrange("p (j c) -> p j c", j=PACK),
                 in_=w1[z * K_PASS : (z + 1) * K_PASS, :].rearrange("(p j) c -> p j c", j=PACK),
             )
-        load_words(1)
-        for t in range(PACK):
-            nc.sync.dma_start(
-                out=w2_raw[t // 2][:, (t % 2) * N : (t % 2 + 1) * N],
-                in_=w2.rearrange("(g t r) c -> t g r c", t=PACK, r=8)[t],
-            )
-        nc.sync.dma_start(dst_sb[:], dst)
-        first = CHUNKS[0][1]
-        nc.sync.dma_start(out=gate_sb[:, :first], in_=gate[:, :first])
-        nc.sync.dma_start(out=gate_sb[:, first:], in_=gate[:, first:])
-        nc.vector.memset(placed[0][:], 0.0)
-        nc.gpsimd.memset(placed[1][:], 0.0)
 
+        nc.sync.dma_start(out=x_rows[:32, :].bitcast(I32), in_=x_scales.rearrange("z b c -> b z c").bitcast(I32))
+        nc.sync.dma_start(offs_sb[:], offs)
+        load_words(0)
+        w1_raw = [tile("w1_raw%d" % z, PACK * H, F32) for z in range(PASSES)]
+        for z in range(PASSES):
+            load_w1(z, w1_raw[z])
+        nc.sync.dma_start(dst_sb[:], dst)
+        nc.vector.memset(x_rows[32:64, :].bitcast(I32), 0)
+        nc.vector.memset(x_rows[64:, :].bitcast(I32), 0)
+        nc.vector.memset(zero[:], 0.0)
+        nc.vector.memset(planes[:].bitcast(I32), 0)
+        for m in range(N // P):
+            nc.scalar.copy(out=placed[m][:], in_=zero[:, 0:1].to_broadcast([P, U]))
+
+        picked_rows = tile("picked_rows", S, U8)
+        nc.vector.tensor_copy(picked_rows[:], x_rows[:].indirect(offs_sb[:]))
+        for q in range(4):
+            nc.sync.dma_start(
+                out=planes[32 * q : 32 * q + 4, :].bitcast(I32).rearrange("p (z c) -> p z c", z=PASSES),
+                in_=picked_rows[8 * q : 8 * q + 8, :].bitcast(I32),
+            )
+        x_table.append(tile_at("x_table1", T, U32, 0))
+        load_words(1)
         words0 = tile("words0", S, U32)
         nc.vector.tensor_copy(words0[:], x_table[0][:].indirect(offs_sb[:]))
-        planes = tile("planes", S, U8)
-        nc.vector.tensor_copy(planes[:], x_planes[:].indirect(offs_sb[:]))
+        words1 = {}
+
+        def gather_words1(lo, hi, offset):
+            piece = tile_at("words1_%d" % lo, hi - lo, U32, offset)
+            nc.vector.tensor_copy(piece[:], x_table[1][:].indirect(entries(offs_sb, lo, hi)))
+            for b0 in range(lo, hi, BLOCK):
+                words1[b0] = piece[:, b0 - lo : b0 - lo + BLOCK]
+
+        def picked_words(z, b0):
+            return words0[:, b0 : b0 + BLOCK] if z == 0 else words1[b0]
+
+        w2_raw = tile_at("w2_raw", PACK * N, F32, 8192)
+        gate_sb = tile_at("gate_sb", S, F32, 12288)
+        for u in range(2):
+            nc.sync.dma_start(
+                out=w2_raw[:, 2 * u * N : (2 * u + 2) * N],
+                in_=w2.rearrange("(g u r e) c -> u g r (e c)", u=2, r=8, e=2)[u],
+            )
+        nc.sync.dma_start(out=gate_sb[:], in_=gate)
 
         w1_codes = [tile("w1_codes%d" % z, H, U32) for z in range(PASSES)]
         w1_scales = [tile("w1_scales%d" % z, H, U8) for z in range(PASSES)]
-
-        def round_w1(engine_copy, z, t, grouped, at):
-            engine_copy(
-                out=grouped[:, at * K_PASS : (at + 1) * K_PASS].rearrange("p (g h i j) -> p g h j i", h=2, i=4, j=PACK),
-                in_=w1_raw[z][:].rearrange("p (j g t h i) -> p t g h j i", j=PACK, t=PACK, h=2, i=4)[:, t],
-            )
-
-        def quantise_w1(z, t0, t1, grouped):
-            cols = slice(t0 * P, t1 * P)
-            nc.vector.quantize_mx(out=w1_codes[z][:, cols].bitcast(FP8X4), scales=w1_scales[z][:, cols], in_=grouped[:])
-
-        grouped0 = tile_at("w1_grouped0", PACK * H, BF16, 2048)
-        for t in range(PACK):
-            round_w1(nc.scalar.copy, 0, t, grouped0, t)
-        quantise_w1(0, 0, PACK, grouped0)
-        halves = [tile_at("w1_grouped1_0", 2 * K_PASS, BF16, 1024), tile("w1_grouped1_1", 2 * K_PASS, BF16)]
-        for t in range(PACK):
-            round_w1(nc.vector.tensor_copy if t < 2 else nc.scalar.copy, 1, t, halves[t // 2], t % 2)
-        for u in (1, 0):
-            quantise_w1(1, 2 * u, 2 * u + 2, halves[u])
+        for z in range(PASSES):
+            grouped = [tile("w1_grouped%d_%d" % (z, t), K_PASS, BF16) for t in range(PACK)]
+            for t in range(PACK):
+                engine_copy = nc.vector.tensor_copy if t < 2 else nc.scalar.copy
+                engine_copy(
+                    out=grouped[t][:].rearrange("p (g h i j) -> p g h j i", h=4, i=2, j=PACK),
+                    in_=w1_raw[z][:].rearrange("p (j g u h i e) -> p u e g h j i", j=PACK, u=2, h=4, i=2, e=2)[:, t // 2, t % 2],
+                )
+            for t in range(PACK):
+                cols = slice(t * P, (t + 1) * P)
+                nc.vector.quantize_mx(out=w1_codes[z][:, cols].bitcast(FP8X4), scales=w1_scales[z][:, cols], in_=grouped[t][:])
 
         banks = {}
 
-        def first_product(z, b0, moving, opens):
-            if opens:
-                banks[b0] = psum.tile([P, PACK * BLOCK], F32, name="bank%d" % (b0 // BLOCK))
-            for t in range(PACK):
-                cols = slice(t * P, (t + 1) * P)
-                nc.tensor.matmul_mx(
-                    out=banks[b0][:, t * BLOCK : (t + 1) * BLOCK],
-                    lhsT=w1_codes[z][:, cols].bitcast(FP8X4),
-                    lhsT_scale=w1_scales[z][:, cols],
-                    rhs=moving.bitcast(FP8X4),
-                    rhs_scale=planes[4 * z :, b0 : b0 + BLOCK],
-                    start=(opens and t == 0),
-                    stop=(not opens and t == PACK - 1),
-                )
-
-        for b0 in range(0, AHEAD, BLOCK):
-            first_product(0, b0, words0[:, b0 : b0 + BLOCK], True)
-
-        def second_pass(lo, words):
-            for at in range(0, words.shape[1], BLOCK):
-                b0 = lo + at
-                first_product(1, b0, words[:, at : at + BLOCK], b0 >= AHEAD)
-                if b0 >= AHEAD:
-                    first_product(0, b0, words0[:, b0 : b0 + BLOCK], False)
-
-        def gather_words1(lo, hi, offset):
-            words = tile_at("words1_%d" % lo, hi - lo, U32, offset)
-            nc.vector.tensor_copy(words[:], x_table[1][:].indirect(entries(offs_sb, lo, hi)))
-            return words[:]
-
-        h_codes, h_scales = [], []
-
-        def hidden(c, grouped):
-            lo, hi = CHUNKS[c]
-            for b0 in range(lo, hi, BLOCK):
-                nc.scalar.activation(
-                    out=grouped[:, PACK * (b0 - lo) : PACK * (b0 - lo + BLOCK)].rearrange("p (n t) -> p n t", t=PACK),
-                    in_=banks[b0][:].rearrange("p (t n) -> p n t", t=PACK),
-                    func=RELU,
-                )
-            codes = tile_at("h_codes%d" % c, hi - lo, U32, 11264 - 4 * lo) if c < 2 else tile("h_codes%d" % c, hi - lo, U32)
-            scales = tile("h_scales%d" % c, hi - lo, U8)
-            nc.vector.quantize_mx(out=codes[:].bitcast(FP8X4), scales=scales[:], in_=grouped[:])
-            h_codes.append(codes)
-            h_scales.append(scales)
-
-        second_pass(0, gather_words1(0, 256, 16384))
-        second_pass(256, gather_words1(256, 768, 17408))
-        w2_grouped = tile("w2_grouped", PACK * N, BF16)
-        for u, engine_copy in enumerate((nc.scalar.copy, nc.vector.tensor_copy)):
-            engine_copy(
-                out=w2_grouped[:].rearrange("p (c i u e) -> p u c e i", i=4, u=2, e=2)[:, u],
-                in_=w2_raw[u][:].rearrange("p (e c i) -> p c e i", i=4, e=2),
+        def first_product(z, t, b0):
+            if z == 0 and t == 0:
+                banks[b0] = psum.tile([P, PACK * BLOCK], F32, name="bank%d" % BLOCK_BANK[b0 // BLOCK])
+            cols = slice(t * P, (t + 1) * P)
+            nc.tensor.matmul_mx(
+                out=banks[b0][:, t * BLOCK : (t + 1) * BLOCK],
+                lhsT=w1_codes[z][:, cols].bitcast(FP8X4),
+                lhsT_scale=w1_scales[z][:, cols],
+                rhs=picked_words(z, b0).bitcast(FP8X4),
+                rhs_scale=planes[:, z * S + b0 : z * S + b0 + BLOCK],
+                start=(z == 0 and t == 0),
+                stop=(z == PASSES - 1 and t == PACK - 1),
             )
-        w2_codes = tile("w2_codes", N, U32)
-        w2_scales = tile("w2_scales", N, U8)
-        nc.vector.quantize_mx(out=w2_codes[:].bitcast(FP8X4), scales=w2_scales[:], in_=w2_grouped[:])
-        hidden(0, tile_at("h_grouped0", 1024, BF16, 8192))
+
+        def products(z, lo, hi):
+            for t in range(PACK):
+                for b0 in range(lo, hi, BLOCK):
+                    first_product(z, t, b0)
+
+        def finish_block(b0):
+            if b0 >= AHEAD:
+                products(0, b0, b0 + BLOCK)
+            products(1, b0, b0 + BLOCK)
+
+        first_grouped = tile_at("first_grouped", PACK * (FIRST + P), BF16, 24576)
+        first_codes = tile("first_codes", FIRST + P, U32)
+        first_scales = tile("first_scales", FIRST + P, U8)
+        w2_grouped = [first_grouped[:, PACK * FIRST :]]
+        w2_codes = [first_codes[:, FIRST:], tile("w2_codes1", P, U32)[:]]
+        w2_scales = [first_scales[:, FIRST:], tile("w2_scales1", P, U8)[:]]
+
+        def round_w2(m, engine_copy):
+            engine_copy(
+                out=w2_grouped[m].rearrange("p (c i t) -> p c t i", i=4, t=PACK),
+                in_=w2_raw[:].rearrange("p (t m c i) -> p m c t i", t=PACK, m=N // P, i=4)[:, m],
+            )
+
+        def quantise_w2(m):
+            nc.vector.quantize_mx(out=w2_codes[m].bitcast(FP8X4), scales=w2_scales[m], in_=w2_grouped[m])
+
+        h_grouped = [first_grouped, tile_at("h_grouped1", PACK * 256, BF16, 17408)]
+        h_codes = [first_codes] + [tile("h_codes%d" % c, CHUNKS[c][1] - CHUNKS[c][0], U32) for c in (1, 2)]
+        h_scales = [first_scales] + [tile("h_scales%d" % c, CHUNKS[c][1] - CHUNKS[c][0], U8) for c in (1, 2)]
+
+        def relu(c, b0, on_vector=False):
+            at = PACK * (b0 - CHUNKS[c][0])
+            rounded = h_grouped[c][:, at : at + PACK * BLOCK].rearrange("p (n t) -> p n t", t=PACK)
+            sums = banks[b0][:].rearrange("p (t n) -> p n t", t=PACK)
+            if on_vector:
+                nc.vector.tensor_scalar_max(rounded, sums, 0.0)
+            else:
+                nc.scalar.activation(out=rounded, in_=sums, func=RELU)
+
+        def quantise_h(c, lo, hi):
+            lo, hi = lo - CHUNKS[c][0], hi - CHUNKS[c][0]
+            nc.vector.quantize_mx(
+                out=h_codes[c][:, lo:hi].bitcast(FP8X4),
+                scales=h_scales[c][:, lo:hi],
+                in_=h_grouped[c][:, PACK * lo : PACK * hi],
+            )
 
         y = [tile("y%d" % m, S, F32) for m in range(N // P)]
 
-        def product(m, c, bank_number):
-            lo, hi = CHUNKS[c]
+        def product(m, c, lo, hi, bank_number):
+            cols = slice(lo - CHUNKS[c][0], hi - CHUNKS[c][0])
             bank = psum.tile([P, PACK * BLOCK], F32, name="bank%d" % bank_number)
             nc.tensor.matmul_mx(
                 out=bank[:, : hi - lo],
-                lhsT=w2_codes[:, m * P : (m + 1) * P].bitcast(FP8X4),
-                lhsT_scale=w2_scales[:, m * P : (m + 1) * P],
-                rhs=h_codes[c][:].bitcast(FP8X4),
-                rhs_scale=h_scales[c][:],
+                lhsT=w2_codes[m].bitcast(FP8X4),
+                lhsT_scale=w2_scales[m],
+                rhs=h_codes[c][:, cols].bitcast(FP8X4),
+                rhs_scale=h_scales[c][:, cols],
                 start=True,
                 stop=True,
             )
@@ -190,19 +204,39 @@ def tile_picked_route2_mlprelu_p_kernel(tc, x_words, x_scales, gate, w1, w2, off
         def place(m, lo, hi):
             nc.vector.tensor_tensor(placed[m][:].indirect(entries(dst_sb, lo, hi)), y[m][:, lo:hi], gate_sb[:, lo:hi], MULT)
 
-        product(0, 0, 6)
-        product(1, 0, 7)
-        second_pass(768, gather_words1(768, S, 8192))
+        products(0, 0, FIRST)
+        products(0, FIRST, AHEAD)
+        gather_words1(0, FIRST, 16384)
+        gather_words1(FIRST, S - FIRST, 21504)
+        round_w2(0, nc.vector.tensor_copy)
+        for b0 in range(0, FIRST, BLOCK):
+            finish_block(b0)
+            relu(0, b0)
+        quantise_h(0, 0, BLOCK)
+        quantise_h(0, BLOCK, FIRST + P)
+        product(0, 0, 0, FIRST, 4)
+        gather_words1(S - FIRST, S, 26624)
+        for b0 in range(*CHUNKS[1], BLOCK):
+            finish_block(b0)
+            relu(1, b0)
+        quantise_h(1, *CHUNKS[1])
         place(0, *CHUNKS[0])
-        hidden(1, tile("h_grouped1", 1024, BF16))
-        place(1, *CHUNKS[0])
-        product(0, 1, 2)
+        product(0, 1, *CHUNKS[1], 5)
+        w2_grouped.append(tile_at("w2_grouped1", PACK * P, BF16, 17408)[:])
+        round_w2(1, nc.scalar.copy)
+        quantise_w2(1)
         place(0, *CHUNKS[1])
-        hidden(2, tile_at("h_grouped2", 2048, BF16, 11264))
-        product(1, 1, 7)
+        product(1, 0, *CHUNKS[0], 0)
+        place(1, *CHUNKS[0])
+        h_grouped.append(tile("h_grouped2", PACK * 512, BF16))
+        for b0 in range(*CHUNKS[2], BLOCK):
+            finish_block(b0)
+            relu(2, b0)
+        quantise_h(2, *CHUNKS[2])
+        product(1, 1, *CHUNKS[1], 3)
         place(1, *CHUNKS[1])
-        product(0, 2, 4)
-        product(1, 2, 5)
+        product(0, 2, *CHUNKS[2], 1)
+        product(1, 2, *CHUNKS[2], 2)
         place(0, *CHUNKS[2])
         nc.sync.dma_start(out=out[:P, :], in_=placed[0][:])
         place(1, *CHUNKS[2])

@@ -59,8 +59,8 @@ def tile_picked_route2_mlprelu_p_kernel(tc, x_words, x_scales, gate, w1, w2, off
 
         def load_w1(z, raw):
             nc.sync.dma_start(
-                out=raw[:].rearrange("p (j c) -> p j c", j=PACK),
-                in_=w1[z * K_PASS : (z + 1) * K_PASS, :].rearrange("(p j) c -> p j c", j=PACK),
+                out=raw[:],
+                in_=w1[z * K_PASS : (z + 1) * K_PASS, :].rearrange("(p j) c -> p (j c)", j=PACK),
             )
 
         nc.sync.dma_start(out=x_rows[:32, :].bitcast(I32), in_=x_scales.rearrange("z b c -> b z c").bitcast(I32))
@@ -148,10 +148,10 @@ def tile_picked_route2_mlprelu_p_kernel(tc, x_words, x_scales, gate, w1, w2, off
                 products(0, b0, b0 + BLOCK)
             products(1, b0, b0 + BLOCK)
 
-        first_grouped = tile_at("first_grouped", PACK * (FIRST + P), BF16, 24576)
+        first_grouped = tile_at("first_grouped", PACK * FIRST, BF16, 24576)
         first_codes = tile("first_codes", FIRST + P, U32)
         first_scales = tile("first_scales", FIRST + P, U8)
-        w2_grouped = [first_grouped[:, PACK * FIRST :]]
+        w2_grouped = [tile("w2_grouped0", PACK * P, BF16)[:]]
         w2_codes = [first_codes[:, FIRST:], tile("w2_codes1", P, U32)[:]]
         w2_scales = [first_scales[:, FIRST:], tile("w2_scales1", P, U8)[:]]
 
@@ -213,9 +213,10 @@ def tile_picked_route2_mlprelu_p_kernel(tc, x_words, x_scales, gate, w1, w2, off
             finish_block(b0)
             relu(0, b0)
         quantise_h(0, 0, BLOCK)
-        quantise_h(0, BLOCK, FIRST + P)
+        quantise_h(0, BLOCK, FIRST)
+        quantise_w2(0)
         product(0, 0, 0, FIRST, 4)
-        gather_words1(S - FIRST, S, 26624)
+        gather_words1(S - FIRST, S, 25600)
         for b0 in range(*CHUNKS[1], BLOCK):
             finish_block(b0)
             relu(1, b0)
@@ -235,8 +236,9 @@ def tile_picked_route2_mlprelu_p_kernel(tc, x_words, x_scales, gate, w1, w2, off
         quantise_h(2, *CHUNKS[2])
         product(1, 1, *CHUNKS[1], 3)
         place(1, *CHUNKS[1])
-        product(0, 2, *CHUNKS[2], 1)
-        product(1, 2, *CHUNKS[2], 2)
+        for m in range(N // P):
+            product(m, 2, 512, 768, 1 + m)
+            product(m, 2, 768, S, 6 + m)
         place(0, *CHUNKS[2])
         nc.sync.dma_start(out=out[:P, :], in_=placed[0][:])
         place(1, *CHUNKS[2])

@@ -22,7 +22,7 @@ PASSES = K // K_PASS
 STRIPE = 16
 BLOCK = 128
 AHEAD = 512
-BLOCK_BANK = (0, 1, 2, 3, 4, 3, 4, 3)
+BLOCK_BANK = (0, 1, 2, 3, 4, 3, 5, 3)
 FIRST = 256
 CHUNKS = ((0, 256), (256, 512), (512, 1024))
 
@@ -45,8 +45,8 @@ def tile_picked_route2_mlprelu_p_kernel(tc, x_words, x_scales, gate, w1, w2, off
 
         offs_sb = tile("offs_sb", S // STRIPE, U16)
         dst_sb = tile("dst_sb", S // STRIPE, U16)
-        x_rows = tile_at("x_rows", T, U8, 0)
-        x_table = [tile_at("x_table0", T, U32, 8192)]
+        x_rows = tile_at("x_rows", 3 * T, U8, 7168)[:, :T]
+        x_table = [tile_at("x_table0", T, U32, 16384)]
         placed = [tile("placed%d" % m, U, F32) for m in range(N // P)]
         planes = tile("planes", PASSES * S, U8)
         zero = tile("zero", 16, F32)
@@ -78,12 +78,16 @@ def tile_picked_route2_mlprelu_p_kernel(tc, x_words, x_scales, gate, w1, w2, off
             nc.scalar.copy(out=placed[m][:], in_=zero[:, 0:1].to_broadcast([P, U]))
 
         picked_rows = tile("picked_rows", S, U8)
-        nc.vector.tensor_copy(picked_rows[:], x_rows[:].indirect(offs_sb[:]))
-        for q in range(4):
-            nc.sync.dma_start(
-                out=planes[32 * q : 32 * q + 4, :].bitcast(I32).rearrange("p (z c) -> p z c", z=PASSES),
-                in_=picked_rows[8 * q : 8 * q + 8, :].bitcast(I32),
-            )
+        nc.vector.tensor_copy(picked_rows[:], x_rows.indirect(offs_sb[:]))
+
+        def move_rows(lo, hi):
+            for q in range(4):
+                nc.sync.dma_start(
+                    out=planes[32 * q : 32 * q + 4, :].bitcast(I32).rearrange("p (z c) -> p z c", z=PASSES)[:, :, lo // 4 : hi // 4],
+                    in_=picked_rows[8 * q : 8 * q + 8, lo:hi].bitcast(I32),
+                )
+
+        move_rows(0, AHEAD)
         x_table.append(tile_at("x_table1", T, U32, 0))
         load_words(1)
         words0 = tile("words0", S, U32)
@@ -107,6 +111,7 @@ def tile_picked_route2_mlprelu_p_kernel(tc, x_words, x_scales, gate, w1, w2, off
                 in_=w2.rearrange("(g u r e) c -> u g r (e c)", u=2, r=8, e=2)[u],
             )
         nc.sync.dma_start(out=gate_sb[:], in_=gate)
+        move_rows(AHEAD, S)
 
         w1_codes = [tile("w1_codes%d" % z, H, U32) for z in range(PASSES)]
         w1_scales = [tile("w1_scales%d" % z, H, U8) for z in range(PASSES)]
@@ -227,10 +232,13 @@ def tile_picked_route2_mlprelu_p_kernel(tc, x_words, x_scales, gate, w1, w2, off
         round_w2(1, nc.scalar.copy)
         quantise_w2(1)
         place(0, *CHUNKS[1])
-        product(1, 0, *CHUNKS[0], 0)
-        place(1, *CHUNKS[0])
         h_grouped.append(tile("h_grouped2", PACK * 512, BF16))
-        for b0 in range(*CHUNKS[2], BLOCK):
+        for b0 in range(512, 768, BLOCK):
+            finish_block(b0)
+            relu(2, b0)
+        product(1, 0, *CHUNKS[0], 4)
+        place(1, *CHUNKS[0])
+        for b0 in range(768, S, BLOCK):
             finish_block(b0)
             relu(2, b0)
         quantise_h(2, *CHUNKS[2])

@@ -21,10 +21,10 @@ K_PASS = P * PACK
 PASSES = K // K_PASS
 STRIPE = 16
 BLOCK = 128
-AHEAD = 512
-BLOCK_BANK = (0, 1, 2, 3, 4, 3, 5, 3)
-FIRST = 256
-CHUNKS = ((0, 256), (256, 512), (512, 1024))
+QUARTER = S // 4
+HALF = S // 2
+WARM_UPS = 4
+BLOCK_BANK = (0, 1, 2, 3, 4, 2, 5, 3)
 
 
 def tile_picked_route2_mlprelu_p_kernel(tc, x_words, x_scales, gate, w1, w2, offs, dst, out):
@@ -40,214 +40,191 @@ def tile_picked_route2_mlprelu_p_kernel(tc, x_words, x_scales, gate, w1, w2, off
         def tile_at(name, width, dtype, offset):
             return reused.tile([P, width], dtype, name=name, align_bytes=64, offset=offset)
 
+        def bank(number):
+            return psum.tile([P, PACK * BLOCK], F32, name="bank%d" % number)
+
         def entries(list_tile, lo, hi):
             return list_tile[:, lo // STRIPE : hi // STRIPE]
 
+        def quantise(codes, scales, values):
+            nc.vector.quantize_mx(out=codes.bitcast(FP8X4), scales=scales, in_=values)
+
+        def multiply(sums, left, left_scales, right, right_scales, start, stop):
+            nc.tensor.matmul_mx(
+                out=sums,
+                lhsT=left.bitcast(FP8X4),
+                lhsT_scale=left_scales,
+                rhs=right.bitcast(FP8X4),
+                rhs_scale=right_scales,
+                start=start,
+                stop=stop,
+            )
+
         offs_sb = tile("offs_sb", S // STRIPE, U16)
         dst_sb = tile("dst_sb", S // STRIPE, U16)
-        x_rows = tile_at("x_rows", 3 * T, U8, 7168)[:, :T]
-        x_table = [tile_at("x_table0", T, U32, 16384)]
-        placed = [tile("placed%d" % m, U, F32) for m in range(N // P)]
+        scale_rows = tile_at("scale_rows", 3 * T, U8, 7168)[:, :T]
+        table0 = tile("table0", T, U32)
+        w1_raw = [tile("w1_raw%d" % z, PACK * H, F32) for z in range(PASSES)]
+        windows = [tile("window%d" % m, U, F32) for m in range(N // P)]
         planes = tile("planes", PASSES * S, U8)
         zero = tile("zero", 16, F32)
 
-        def load_words(z):
-            nc.sync.dma_start(
-                out=x_table[z][:].bitcast(I32),
-                in_=x_words[z].rearrange("p c r -> p (c r)").bitcast(I32),
-            )
+        def load_table(table, z):
+            nc.sync.dma_start(out=table[:].bitcast(I32), in_=x_words[z].rearrange("p c r -> p (c r)").bitcast(I32))
 
-        def load_w1(z, raw):
-            nc.sync.dma_start(
-                out=raw[:],
-                in_=w1[z * K_PASS : (z + 1) * K_PASS, :].rearrange("(p j) c -> p (j c)", j=PACK),
-            )
-
-        nc.sync.dma_start(out=x_rows[:32, :].bitcast(I32), in_=x_scales.rearrange("z b c -> b z c").bitcast(I32))
+        nc.sync.dma_start(out=scale_rows[:32, :].bitcast(I32), in_=x_scales.rearrange("z b c -> b z c").bitcast(I32))
         nc.sync.dma_start(offs_sb[:], offs)
-        load_words(0)
-        w1_raw = [tile("w1_raw%d" % z, PACK * H, F32) for z in range(PASSES)]
+        load_table(table0, 0)
         for z in range(PASSES):
-            load_w1(z, w1_raw[z])
+            rows = w1[z * K_PASS : (z + 1) * K_PASS, :]
+            nc.sync.dma_start(out=w1_raw[z][:], in_=rows.rearrange("(p j) c -> p (j c)", j=PACK))
         nc.sync.dma_start(dst_sb[:], dst)
-        nc.vector.memset(x_rows[32:64, :].bitcast(I32), 0)
-        nc.vector.memset(x_rows[64:, :].bitcast(I32), 0)
+        nc.vector.memset(scale_rows[32:64, :].bitcast(I32), 0)
+        nc.vector.memset(scale_rows[64:, :].bitcast(I32), 0)
         nc.vector.memset(zero[:], 0.0)
         nc.vector.memset(planes[:].bitcast(I32), 0)
-        for m in range(N // P):
-            nc.scalar.copy(out=placed[m][:], in_=zero[:, 0:1].to_broadcast([P, U]))
+        for window in windows:
+            nc.scalar.copy(out=window[:], in_=zero[:, 0:1].to_broadcast([P, U]))
 
         picked_rows = tile("picked_rows", S, U8)
-        nc.vector.tensor_copy(picked_rows[:], x_rows.indirect(offs_sb[:]))
+        nc.vector.tensor_copy(picked_rows[:], scale_rows.indirect(offs_sb[:]))
 
         def move_rows(lo, hi):
             for q in range(4):
-                nc.sync.dma_start(
-                    out=planes[32 * q : 32 * q + 4, :].bitcast(I32).rearrange("p (z c) -> p z c", z=PASSES)[:, :, lo // 4 : hi // 4],
-                    in_=picked_rows[8 * q : 8 * q + 8, lo:hi].bitcast(I32),
-                )
+                both = planes[32 * q : 32 * q + 4, :].bitcast(I32).rearrange("p (z c) -> p z c", z=PASSES)
+                nc.sync.dma_start(out=both[:, :, lo // 4 : hi // 4], in_=picked_rows[8 * q : 8 * q + 8, lo:hi].bitcast(I32))
 
-        move_rows(0, AHEAD)
-        x_table.append(tile_at("x_table1", T, U32, 0))
-        load_words(1)
-        words0 = tile("words0", S, U32)
-        nc.vector.tensor_copy(words0[:], x_table[0][:].indirect(offs_sb[:]))
-        words1 = {}
-
-        def gather_words1(lo, hi, offset):
-            piece = tile_at("words1_%d" % lo, hi - lo, U32, offset)
-            nc.vector.tensor_copy(piece[:], x_table[1][:].indirect(entries(offs_sb, lo, hi)))
-            for b0 in range(lo, hi, BLOCK):
-                words1[b0] = piece[:, b0 - lo : b0 - lo + BLOCK]
-
-        def picked_words(z, b0):
-            return words0[:, b0 : b0 + BLOCK] if z == 0 else words1[b0]
-
-        w2_raw = tile_at("w2_raw", PACK * N, F32, 8192)
+        move_rows(0, HALF)
+        table1 = tile_at("table1", T, U32, 0)
+        load_table(table1, 1)
+        w2_raw = [tile_at("w2_raw%d" % m, PACK * P, F32, 8192 + 2048 * m) for m in range(N // P)]
+        for m in range(N // P):
+            columns = w2[:, m * P : (m + 1) * P].rearrange("(p t) c -> p t c", t=PACK)
+            nc.sync.dma_start(out=w2_raw[m][:].rearrange("p (t c) -> p t c", t=PACK), in_=columns)
         gate_sb = tile_at("gate_sb", S, F32, 12288)
-        for u in range(2):
-            nc.sync.dma_start(
-                out=w2_raw[:, 2 * u * N : (2 * u + 2) * N],
-                in_=w2.rearrange("(g u r e) c -> u g r (e c)", u=2, r=8, e=2)[u],
-            )
         nc.sync.dma_start(out=gate_sb[:], in_=gate)
-        move_rows(AHEAD, S)
+        move_rows(HALF, S)
+
+        words0 = tile("words0", S, U32)
+        nc.vector.tensor_copy(words0[:], table0[:].indirect(offs_sb[:]))
 
         w1_codes = [tile("w1_codes%d" % z, H, U32) for z in range(PASSES)]
         w1_scales = [tile("w1_scales%d" % z, H, U8) for z in range(PASSES)]
         for z in range(PASSES):
-            grouped = [tile("w1_grouped%d_%d" % (z, t), K_PASS, BF16) for t in range(PACK)]
-            for t in range(PACK):
-                engine_copy = nc.vector.tensor_copy if t < 2 else nc.scalar.copy
+            rounded = [tile("w1_rounded%d_%d" % (z, u), 2 * K_PASS, BF16) for u in range(2)]
+            for u, engine_copy in enumerate((nc.vector.tensor_copy, nc.scalar.copy)):
                 engine_copy(
-                    out=grouped[t][:].rearrange("p (g h i j) -> p g h j i", h=4, i=2, j=PACK),
-                    in_=w1_raw[z][:].rearrange("p (j g u h i e) -> p u e g h j i", j=PACK, u=2, h=4, i=2, e=2)[:, t // 2, t % 2],
+                    out=rounded[u][:].rearrange("p (e m j) -> p m j e", e=2, j=PACK),
+                    in_=w1_raw[z][:].rearrange("p (j m u e) -> p u m j e", j=PACK, u=2, e=2)[:, u],
                 )
-            for t in range(PACK):
-                cols = slice(t * P, (t + 1) * P)
-                nc.vector.quantize_mx(out=w1_codes[z][:, cols].bitcast(FP8X4), scales=w1_scales[z][:, cols], in_=grouped[t][:])
+            for u in range(2):
+                cols = slice(2 * u * P, (2 * u + 2) * P)
+                quantise(w1_codes[z][:, cols], w1_scales[z][:, cols], rounded[u][:])
 
-        banks = {}
+        spare = bank(7)
+        for turn in range(WARM_UPS):
+            multiply(spare[:, : 2 * P], w1_codes[0][:, :P], w1_scales[0][:, :P], w1_codes[0][:, : 2 * P], w1_scales[0][:, : 2 * P], True, True)
 
-        def first_product(z, t, b0):
+        words1 = {}
+
+        def gather_words1(quarter, piece):
+            lo = quarter * QUARTER
+            nc.vector.tensor_copy(piece[:], table1[:].indirect(entries(offs_sb, lo, lo + QUARTER)))
+            for b in range(2):
+                words1[2 * quarter + b] = piece[:, b * BLOCK : (b + 1) * BLOCK]
+
+        sums = {}
+
+        def first_product(z, t, b):
             if z == 0 and t == 0:
-                banks[b0] = psum.tile([P, PACK * BLOCK], F32, name="bank%d" % BLOCK_BANK[b0 // BLOCK])
+                sums[b] = bank(BLOCK_BANK[b])
             cols = slice(t * P, (t + 1) * P)
-            nc.tensor.matmul_mx(
-                out=banks[b0][:, t * BLOCK : (t + 1) * BLOCK],
-                lhsT=w1_codes[z][:, cols].bitcast(FP8X4),
-                lhsT_scale=w1_scales[z][:, cols],
-                rhs=picked_words(z, b0).bitcast(FP8X4),
-                rhs_scale=planes[:, z * S + b0 : z * S + b0 + BLOCK],
-                start=(z == 0 and t == 0),
-                stop=(z == PASSES - 1 and t == PACK - 1),
-            )
+            words = words0[:, b * BLOCK : (b + 1) * BLOCK] if z == 0 else words1[b]
+            plane = planes[:, z * S + b * BLOCK : z * S + (b + 1) * BLOCK]
+            first, last = (z, t) == (0, 0), (z, t) == (PASSES - 1, PACK - 1)
+            multiply(sums[b][:, t * BLOCK : (t + 1) * BLOCK], w1_codes[z][:, cols], w1_scales[z][:, cols], words, plane, first, last)
 
-        def products(z, lo, hi):
+        for pair in ((0, 1), (2, 3)):
             for t in range(PACK):
-                for b0 in range(lo, hi, BLOCK):
-                    first_product(z, t, b0)
+                for b in pair:
+                    first_product(0, t, b)
 
-        def finish_block(b0):
-            if b0 >= AHEAD:
-                products(0, b0, b0 + BLOCK)
-            products(1, b0, b0 + BLOCK)
+        h_codes = [tile("h_codes%d" % c, width, U32) for c, width in enumerate((QUARTER, QUARTER, HALF))]
+        h_scales = [tile("h_scales%d" % c, width, U8) for c, width in enumerate((QUARTER, QUARTER, HALF))]
+        block0 = tile_at("block0", PACK * BLOCK, BF16, 16384)
+        block1 = tile("block1", PACK * BLOCK, BF16)
+        h_second = tile("h_second", PACK * QUARTER, BF16)
+        h_rest = tile("h_rest", PACK * HALF, BF16)
+        h_rounded = [block0[:], block1[:]]
+        h_rounded.extend(h_second[:, PACK * BLOCK * b : PACK * BLOCK * (b + 1)] for b in range(2))
+        h_rounded.extend(h_rest[:, PACK * BLOCK * b : PACK * BLOCK * (b + 1)] for b in range(4))
 
-        first_grouped = tile_at("first_grouped", PACK * FIRST, BF16, 24576)
-        first_codes = tile("first_codes", FIRST + P, U32)
-        first_scales = tile("first_scales", FIRST + P, U8)
-        w2_grouped = [tile("w2_grouped0", PACK * P, BF16)[:]]
-        w2_codes = [first_codes[:, FIRST:], tile("w2_codes1", P, U32)[:]]
-        w2_scales = [first_scales[:, FIRST:], tile("w2_scales1", P, U8)[:]]
+        def finish_block(b, on_vector=False):
+            for z in range(0 if b * BLOCK >= HALF else 1, PASSES):
+                for t in range(PACK):
+                    first_product(z, t, b)
+            rounded = h_rounded[b].rearrange("p (n t) -> p n t", t=PACK)
+            block_sums = sums[b][:].rearrange("p (t n) -> p n t", t=PACK)
+            if on_vector:
+                nc.vector.tensor_scalar_max(rounded, block_sums, 0.0)
+            else:
+                nc.scalar.activation(out=rounded, in_=block_sums, func=RELU)
 
-        def round_w2(m, engine_copy):
-            engine_copy(
-                out=w2_grouped[m].rearrange("p (c i t) -> p c t i", i=4, t=PACK),
-                in_=w2_raw[:].rearrange("p (t m c i) -> p m c t i", t=PACK, m=N // P, i=4)[:, m],
+        w2_codes = [tile("w2_codes%d" % m, P, U32) for m in range(N // P)]
+        w2_scales = [tile("w2_scales%d" % m, P, U8) for m in range(N // P)]
+        w2_rounded = [tile("w2_rounded%d" % m, PACK * P, BF16) for m in range(N // P)]
+
+        def round_w2(m):
+            nc.scalar.copy(
+                out=w2_rounded[m][:].rearrange("p (c i t) -> p c t i", i=4, t=PACK),
+                in_=w2_raw[m][:].rearrange("p (t c i) -> p c t i", t=PACK, i=4),
             )
 
         def quantise_w2(m):
-            nc.vector.quantize_mx(out=w2_codes[m].bitcast(FP8X4), scales=w2_scales[m], in_=w2_grouped[m])
-
-        h_grouped = [first_grouped, tile_at("h_grouped1", PACK * 256, BF16, 17408)]
-        h_codes = [first_codes] + [tile("h_codes%d" % c, CHUNKS[c][1] - CHUNKS[c][0], U32) for c in (1, 2)]
-        h_scales = [first_scales] + [tile("h_scales%d" % c, CHUNKS[c][1] - CHUNKS[c][0], U8) for c in (1, 2)]
-
-        def relu(c, b0, on_vector=False):
-            at = PACK * (b0 - CHUNKS[c][0])
-            rounded = h_grouped[c][:, at : at + PACK * BLOCK].rearrange("p (n t) -> p n t", t=PACK)
-            sums = banks[b0][:].rearrange("p (t n) -> p n t", t=PACK)
-            if on_vector:
-                nc.vector.tensor_scalar_max(rounded, sums, 0.0)
-            else:
-                nc.scalar.activation(out=rounded, in_=sums, func=RELU)
-
-        def quantise_h(c, lo, hi):
-            lo, hi = lo - CHUNKS[c][0], hi - CHUNKS[c][0]
-            nc.vector.quantize_mx(
-                out=h_codes[c][:, lo:hi].bitcast(FP8X4),
-                scales=h_scales[c][:, lo:hi],
-                in_=h_grouped[c][:, PACK * lo : PACK * hi],
-            )
+            quantise(w2_codes[m][:], w2_scales[m][:], w2_rounded[m][:])
 
         y = [tile("y%d" % m, S, F32) for m in range(N // P)]
 
-        def product(m, c, lo, hi, bank_number):
-            cols = slice(lo - CHUNKS[c][0], hi - CHUNKS[c][0])
-            bank = psum.tile([P, PACK * BLOCK], F32, name="bank%d" % bank_number)
-            nc.tensor.matmul_mx(
-                out=bank[:, : hi - lo],
-                lhsT=w2_codes[m].bitcast(FP8X4),
-                lhsT_scale=w2_scales[m],
-                rhs=h_codes[c][:, cols].bitcast(FP8X4),
-                rhs_scale=h_scales[c][:, cols],
-                start=True,
-                stop=True,
-            )
-            nc.scalar.copy(out=y[m][:, lo:hi], in_=bank[:, : hi - lo])
+        def second_product(m, quarter, bank_number):
+            c = min(quarter, 2)
+            cols = slice(QUARTER, HALF) if quarter == 3 else slice(0, QUARTER)
+            product = bank(bank_number)
+            multiply(product[:, :QUARTER], w2_codes[m][:], w2_scales[m][:], h_codes[c][:, cols], h_scales[c][:, cols], True, True)
+            nc.scalar.copy(out=y[m][:, quarter * QUARTER : (quarter + 1) * QUARTER], in_=product[:, :QUARTER])
 
         def place(m, lo, hi):
-            nc.vector.tensor_tensor(placed[m][:].indirect(entries(dst_sb, lo, hi)), y[m][:, lo:hi], gate_sb[:, lo:hi], MULT)
+            nc.vector.tensor_tensor(windows[m][:].indirect(entries(dst_sb, lo, hi)), y[m][:, lo:hi], gate_sb[:, lo:hi], MULT)
 
-        products(0, 0, FIRST)
-        products(0, FIRST, AHEAD)
-        gather_words1(0, FIRST, 16384)
-        gather_words1(FIRST, S - FIRST, 21504)
-        round_w2(0, nc.vector.tensor_copy)
-        for b0 in range(0, FIRST, BLOCK):
-            finish_block(b0)
-            relu(0, b0)
-        quantise_h(0, 0, BLOCK)
-        quantise_h(0, BLOCK, FIRST)
+        for quarter in range(3):
+            gather_words1(quarter, tile("words1_%d" % quarter, QUARTER, U32))
+        round_w2(0)
         quantise_w2(0)
-        product(0, 0, 0, FIRST, 4)
-        gather_words1(S - FIRST, S, 25600)
-        for b0 in range(*CHUNKS[1], BLOCK):
-            finish_block(b0)
-            relu(1, b0)
-        quantise_h(1, *CHUNKS[1])
-        place(0, *CHUNKS[0])
-        product(0, 1, *CHUNKS[1], 5)
-        w2_grouped.append(tile_at("w2_grouped1", PACK * P, BF16, 17408)[:])
-        round_w2(1, nc.scalar.copy)
+        finish_block(0)
+        finish_block(1, on_vector=True)
+        quantise(h_codes[0][:, :BLOCK], h_scales[0][:, :BLOCK], block0[:])
+        quantise(h_codes[0][:, BLOCK:], h_scales[0][:, BLOCK:], block1[:])
+        round_w2(1)
+        gather_words1(3, tile_at("words1_3", QUARTER, U32, 16384))
         quantise_w2(1)
-        place(0, *CHUNKS[1])
-        h_grouped.append(tile("h_grouped2", PACK * 512, BF16))
-        for b0 in range(512, 768, BLOCK):
-            finish_block(b0)
-            relu(2, b0)
-        product(1, 0, *CHUNKS[0], 4)
-        place(1, *CHUNKS[0])
-        for b0 in range(768, S, BLOCK):
-            finish_block(b0)
-            relu(2, b0)
-        quantise_h(2, *CHUNKS[2])
-        product(1, 1, *CHUNKS[1], 3)
-        place(1, *CHUNKS[1])
+        finish_block(2)
+        second_product(0, 0, 4)
+        place(0, 0, QUARTER)
+        finish_block(3)
+        second_product(1, 0, 5)
+        quantise(h_codes[1][:], h_scales[1][:], h_second[:])
+        place(1, 0, QUARTER)
+        finish_block(4)
+        finish_block(5)
+        second_product(0, 1, 4)
+        place(0, QUARTER, HALF)
+        finish_block(6)
+        finish_block(7)
+        quantise(h_codes[2][:], h_scales[2][:], h_rest[:])
+        second_product(1, 1, 3)
+        place(1, QUARTER, HALF)
         for m in range(N // P):
-            product(m, 2, 512, 768, 1 + m)
-            product(m, 2, 768, S, 6 + m)
-        place(0, *CHUNKS[2])
-        nc.sync.dma_start(out=out[:P, :], in_=placed[0][:])
-        place(1, *CHUNKS[2])
-        nc.sync.dma_start(out=out[P:, :], in_=placed[1][:])
+            second_product(m, 2, m)
+            second_product(m, 3, 6 + m)
+        for m in range(N // P):
+            place(m, HALF, S)
+            nc.sync.dma_start(out=out[m * P : (m + 1) * P, :], in_=windows[m][:])

@@ -127,11 +127,11 @@ def tile_picked_route2_mlprelu_p_kernel(tc, x_words, x_scales, gate, w1, w2, off
 
         words1 = {}
 
-        def gather_words1(quarter, piece):
-            lo = quarter * QUARTER
-            nc.vector.tensor_copy(piece[:], table1[:].indirect(entries(offs_sb, lo, lo + QUARTER)))
-            for b in range(2):
-                words1[2 * quarter + b] = piece[:, b * BLOCK : (b + 1) * BLOCK]
+        def gather_words1(lo, hi):
+            piece = tile("words1_%d" % lo, hi - lo, U32)
+            nc.vector.tensor_copy(piece[:], table1[:].indirect(entries(offs_sb, lo, hi)))
+            for at in range(lo, hi, BLOCK):
+                words1[at // BLOCK] = piece[:, at - lo : at - lo + BLOCK]
 
         sums = {}
 
@@ -151,12 +151,11 @@ def tile_picked_route2_mlprelu_p_kernel(tc, x_words, x_scales, gate, w1, w2, off
 
         h_codes = [tile("h_codes%d" % c, width, U32) for c, width in enumerate((QUARTER, QUARTER, HALF))]
         h_scales = [tile("h_scales%d" % c, width, U8) for c, width in enumerate((QUARTER, QUARTER, HALF))]
-        block0 = tile_at("block0", PACK * BLOCK, BF16, 16384)
+        block0 = tile("block0", PACK * BLOCK, BF16)
         block1 = tile("block1", PACK * BLOCK, BF16)
-        h_second = tile("h_second", PACK * QUARTER, BF16)
         h_rest = tile("h_rest", PACK * HALF, BF16)
         h_rounded = [block0[:], block1[:]]
-        h_rounded.extend(h_second[:, PACK * BLOCK * b : PACK * BLOCK * (b + 1)] for b in range(2))
+        h_rounded.extend([None, None])
         h_rounded.extend(h_rest[:, PACK * BLOCK * b : PACK * BLOCK * (b + 1)] for b in range(4))
 
         def finish_block(b, on_vector=False):
@@ -172,10 +171,10 @@ def tile_picked_route2_mlprelu_p_kernel(tc, x_words, x_scales, gate, w1, w2, off
 
         w2_codes = [tile("w2_codes%d" % m, P, U32) for m in range(N // P)]
         w2_scales = [tile("w2_scales%d" % m, P, U8) for m in range(N // P)]
-        w2_rounded = [tile("w2_rounded%d" % m, PACK * P, BF16) for m in range(N // P)]
+        w2_rounded = [tile("w2_rounded0", PACK * P, BF16)]
 
-        def round_w2(m):
-            nc.scalar.copy(
+        def round_w2(m, engine_copy):
+            engine_copy(
                 out=w2_rounded[m][:].rearrange("p (c i t) -> p c t i", i=4, t=PACK),
                 in_=w2_raw[m][:].rearrange("p (t c i) -> p c t i", t=PACK, i=4),
             )
@@ -192,23 +191,32 @@ def tile_picked_route2_mlprelu_p_kernel(tc, x_words, x_scales, gate, w1, w2, off
             multiply(product[:, :QUARTER], w2_codes[m][:], w2_scales[m][:], h_codes[c][:, cols], h_scales[c][:, cols], True, True)
             nc.scalar.copy(out=y[m][:, quarter * QUARTER : (quarter + 1) * QUARTER], in_=product[:, :QUARTER])
 
+        def first_y(b, bank_number):
+            cols = slice(b * BLOCK, (b + 1) * BLOCK)
+            product = bank(bank_number)
+            multiply(product[:, :BLOCK], w2_codes[0][:], w2_scales[0][:], h_codes[0][:, cols], h_scales[0][:, cols], True, True)
+            nc.scalar.copy(out=y[0][:, cols], in_=product[:, :BLOCK])
+
         def place(m, lo, hi):
             nc.vector.tensor_tensor(windows[m][:].indirect(entries(dst_sb, lo, hi)), y[m][:, lo:hi], gate_sb[:, lo:hi], MULT)
 
-        for quarter in range(3):
-            gather_words1(quarter, tile("words1_%d" % quarter, QUARTER, U32))
-        round_w2(0)
+        for lo, hi in ((0, QUARTER), (QUARTER, HALF), (HALF, S)):
+            gather_words1(lo, hi)
+        round_w2(0, nc.scalar.copy)
         quantise_w2(0)
         finish_block(0)
-        finish_block(1, on_vector=True)
+        finish_block(1)
         quantise(h_codes[0][:, :BLOCK], h_scales[0][:, :BLOCK], block0[:])
         quantise(h_codes[0][:, BLOCK:], h_scales[0][:, BLOCK:], block1[:])
-        round_w2(1)
-        gather_words1(3, tile_at("words1_3", QUARTER, U32, 16384))
+        w2_rounded.append(tile_at("w2_rounded1", PACK * P, BF16, 16896))
+        round_w2(1, nc.scalar.copy)
         quantise_w2(1)
-        finish_block(2)
-        second_product(0, 0, 4)
+        first_y(0, 6)
+        first_y(1, 4)
         place(0, 0, QUARTER)
+        h_second = tile_at("h_second", PACK * QUARTER, BF16, 16384)
+        h_rounded[2:4] = [h_second[:, PACK * BLOCK * b : PACK * BLOCK * (b + 1)] for b in range(2)]
+        finish_block(2)
         finish_block(3)
         second_product(1, 0, 5)
         quantise(h_codes[1][:], h_scales[1][:], h_second[:])

@@ -13,6 +13,7 @@ U16 = mybir.dt.uint16
 U8 = mybir.dt.uint8
 FP8X4 = mybir.dt.float8_e4m3fn_x4
 RELU = mybir.ActivationFunctionType.Relu
+COPY = mybir.ActivationFunctionType.Copy
 MULT = mybir.AluOpType.mult
 
 P = 128
@@ -21,10 +22,10 @@ K_PASS = P * PACK
 PASSES = K // K_PASS
 STRIPE = 16
 BLOCK = 128
+BLOCKS = S // BLOCK
 QUARTER = S // 4
 HALF = S // 2
-WARM_UPS = 4
-BLOCK_BANK = (0, 1, 2, 3, 4, 2, 5, 3)
+AHEAD = 6
 
 
 def tile_picked_route2_mlprelu_p_kernel(tc, x_words, x_scales, gate, w1, w2, offs, dst, out):
@@ -89,12 +90,10 @@ def tile_picked_route2_mlprelu_p_kernel(tc, x_words, x_scales, gate, w1, w2, off
         picked_rows = tile("picked_rows", S, U8)
         nc.vector.tensor_copy(picked_rows[:], scale_rows.indirect(offs_sb[:]))
 
-        def move_rows(lo, hi):
-            for q in range(4):
-                both = planes[32 * q : 32 * q + 4, :].bitcast(I32).rearrange("p (z c) -> p z c", z=PASSES)
-                nc.sync.dma_start(out=both[:, :, lo // 4 : hi // 4], in_=picked_rows[8 * q : 8 * q + 8, lo:hi].bitcast(I32))
+        for q in range(4):
+            both = planes[32 * q : 32 * q + 4, :].bitcast(I32).rearrange("p (z c) -> p z c", z=PASSES)
+            nc.sync.dma_start(out=both, in_=picked_rows[8 * q : 8 * q + 8, :].bitcast(I32))
 
-        move_rows(0, HALF)
         table1 = tile_at("table1", T, U32, 0)
         load_table(table1, 1)
         w2_raw = [tile_at("w2_raw%d" % m, PACK * P, F32, 8192 + 2048 * m) for m in range(N // P)]
@@ -103,7 +102,6 @@ def tile_picked_route2_mlprelu_p_kernel(tc, x_words, x_scales, gate, w1, w2, off
             nc.sync.dma_start(out=w2_raw[m][:].rearrange("p (t c) -> p t c", t=PACK), in_=columns)
         gate_sb = tile_at("gate_sb", S, F32, 12288)
         nc.sync.dma_start(out=gate_sb[:], in_=gate)
-        move_rows(HALF, S)
 
         words0 = tile("words0", S, U32)
         nc.vector.tensor_copy(words0[:], table0[:].indirect(offs_sb[:]))
@@ -121,10 +119,6 @@ def tile_picked_route2_mlprelu_p_kernel(tc, x_words, x_scales, gate, w1, w2, off
                 cols = slice(2 * u * P, (2 * u + 2) * P)
                 quantise(w1_codes[z][:, cols], w1_scales[z][:, cols], rounded[u][:])
 
-        spare = bank(7)
-        for turn in range(WARM_UPS):
-            multiply(spare[:, : 2 * P], w1_codes[0][:, :P], w1_scales[0][:, :P], w1_codes[0][:, : 2 * P], w1_scales[0][:, : 2 * P], True, True)
-
         words1 = {}
 
         def gather_words1(lo, hi):
@@ -137,102 +131,86 @@ def tile_picked_route2_mlprelu_p_kernel(tc, x_words, x_scales, gate, w1, w2, off
 
         def first_product(z, t, b):
             if z == 0 and t == 0:
-                sums[b] = bank(BLOCK_BANK[b])
+                sums[b] = bank(b % AHEAD)
             cols = slice(t * P, (t + 1) * P)
             words = words0[:, b * BLOCK : (b + 1) * BLOCK] if z == 0 else words1[b]
             plane = planes[:, z * S + b * BLOCK : z * S + (b + 1) * BLOCK]
             first, last = (z, t) == (0, 0), (z, t) == (PASSES - 1, PACK - 1)
             multiply(sums[b][:, t * BLOCK : (t + 1) * BLOCK], w1_codes[z][:, cols], w1_scales[z][:, cols], words, plane, first, last)
 
-        for pair in ((0, 1), (2, 3)):
-            for t in range(PACK):
-                for b in pair:
-                    first_product(0, t, b)
+        for t in range(PACK):
+            for b in range(AHEAD):
+                first_product(0, t, b)
 
-        h_codes = [tile("h_codes%d" % c, width, U32) for c, width in enumerate((QUARTER, QUARTER, HALF))]
-        h_scales = [tile("h_scales%d" % c, width, U8) for c, width in enumerate((QUARTER, QUARTER, HALF))]
-        block0 = tile("block0", PACK * BLOCK, BF16)
-        block1 = tile("block1", PACK * BLOCK, BF16)
-        h_rest = tile("h_rest", PACK * HALF, BF16)
-        h_rounded = [block0[:], block1[:]]
-        h_rounded.extend([None, None])
-        h_rounded.extend(h_rest[:, PACK * BLOCK * b : PACK * BLOCK * (b + 1)] for b in range(4))
+        for lo, hi in ((0, BLOCK), (BLOCK, QUARTER), (QUARTER, HALF), (HALF, S)):
+            gather_words1(lo, hi)
 
-        def finish_block(b, on_vector=False):
-            for z in range(0 if b * BLOCK >= HALF else 1, PASSES):
-                for t in range(PACK):
-                    first_product(z, t, b)
-            rounded = h_rounded[b].rearrange("p (n t) -> p n t", t=PACK)
-            block_sums = sums[b][:].rearrange("p (t n) -> p n t", t=PACK)
-            if on_vector:
-                nc.vector.tensor_scalar_max(rounded, block_sums, 0.0)
-            else:
-                nc.scalar.activation(out=rounded, in_=block_sums, func=RELU)
+        h_codes = [tile("h_codes%d" % c, QUARTER, U32) for c in range(4)]
+        h_scales = [tile("h_scales%d" % c, QUARTER, U8) for c in range(4)]
+        h_rounded = [tile_at("h_rounded0", PACK * QUARTER, BF16, 16384)]
+        h_rounded.extend(tile("h_rounded%d" % c, PACK * QUARTER, BF16) for c in range(1, 4))
+
+        def hidden(c):
+            for b in (2 * c, 2 * c + 1):
+                for z in range(1 if b < AHEAD else 0, PASSES):
+                    for t in range(PACK):
+                        first_product(z, t, b)
+                at = PACK * BLOCK * (b % 2)
+                rounded = h_rounded[c][:, at : at + PACK * BLOCK].rearrange("p (n t) -> p n t", t=PACK)
+                nc.scalar.activation(out=rounded, in_=sums[b][:].rearrange("p (t n) -> p n t", t=PACK), func=RELU)
+            quantise(h_codes[c][:], h_scales[c][:], h_rounded[c][:])
 
         w2_codes = [tile("w2_codes%d" % m, P, U32) for m in range(N // P)]
         w2_scales = [tile("w2_scales%d" % m, P, U8) for m in range(N // P)]
-        w2_rounded = [tile("w2_rounded0", PACK * P, BF16)]
 
-        def round_w2(m, engine_copy):
+        def prepare_w2(m, rounded, engine_copy):
             engine_copy(
-                out=w2_rounded[m][:].rearrange("p (c i t) -> p c t i", i=4, t=PACK),
+                out=rounded[:].rearrange("p (c i t) -> p c t i", i=4, t=PACK),
                 in_=w2_raw[m][:].rearrange("p (t c i) -> p c t i", t=PACK, i=4),
             )
-
-        def quantise_w2(m):
-            quantise(w2_codes[m][:], w2_scales[m][:], w2_rounded[m][:])
+            quantise(w2_codes[m][:], w2_scales[m][:], rounded[:])
 
         y = [tile("y%d" % m, S, F32) for m in range(N // P)]
+        y_bank = (6, 2, 4, 6)
 
-        def second_product(m, quarter, bank_number):
-            c = min(quarter, 2)
-            cols = slice(QUARTER, HALF) if quarter == 3 else slice(0, QUARTER)
-            product = bank(bank_number)
-            multiply(product[:, :QUARTER], w2_codes[m][:], w2_scales[m][:], h_codes[c][:, cols], h_scales[c][:, cols], True, True)
-            nc.scalar.copy(out=y[m][:, quarter * QUARTER : (quarter + 1) * QUARTER], in_=product[:, :QUARTER])
+        def second_product(m, c):
+            cols = slice(c * QUARTER, (c + 1) * QUARTER)
+            product = bank(y_bank[c] + m)
+            multiply(product[:, :QUARTER], w2_codes[m][:], w2_scales[m][:], h_codes[c][:], h_scales[c][:], True, True)
+            if m == 0:
+                nc.scalar.copy(out=y[0][:, cols], in_=product[:, :QUARTER])
+            else:
+                nc.vector.tensor_tensor(y[1][:, cols], product[:, :QUARTER], gate_sb[:, cols], MULT)
 
-        def first_y(b, bank_number):
-            cols = slice(b * BLOCK, (b + 1) * BLOCK)
-            product = bank(bank_number)
-            multiply(product[:, :BLOCK], w2_codes[0][:], w2_scales[0][:], h_codes[0][:, cols], h_scales[0][:, cols], True, True)
-            nc.scalar.copy(out=y[0][:, cols], in_=product[:, :BLOCK])
+        def place(m, c):
+            lo, hi = c * QUARTER, (c + 1) * QUARTER
+            target = windows[m][:].indirect(entries(dst_sb, lo, hi))
+            if m == 0:
+                nc.vector.tensor_tensor(target, y[0][:, lo:hi], gate_sb[:, lo:hi], MULT)
+            else:
+                nc.scalar.activation(out=target, in_=y[1][:, lo:hi], func=COPY)
 
-        def place(m, lo, hi):
-            nc.vector.tensor_tensor(windows[m][:].indirect(entries(dst_sb, lo, hi)), y[m][:, lo:hi], gate_sb[:, lo:hi], MULT)
-
-        for lo, hi in ((0, QUARTER), (QUARTER, HALF), (HALF, S)):
-            gather_words1(lo, hi)
-        round_w2(0, nc.scalar.copy)
-        quantise_w2(0)
-        finish_block(0)
-        finish_block(1)
-        quantise(h_codes[0][:, :BLOCK], h_scales[0][:, :BLOCK], block0[:])
-        quantise(h_codes[0][:, BLOCK:], h_scales[0][:, BLOCK:], block1[:])
-        w2_rounded.append(tile_at("w2_rounded1", PACK * P, BF16, 16896))
-        round_w2(1, nc.scalar.copy)
-        quantise_w2(1)
-        first_y(0, 6)
-        first_y(1, 4)
-        place(0, 0, QUARTER)
-        h_second = tile_at("h_second", PACK * QUARTER, BF16, 16384)
-        h_rounded[2:4] = [h_second[:, PACK * BLOCK * b : PACK * BLOCK * (b + 1)] for b in range(2)]
-        finish_block(2)
-        finish_block(3)
-        second_product(1, 0, 5)
-        quantise(h_codes[1][:], h_scales[1][:], h_second[:])
-        place(1, 0, QUARTER)
-        finish_block(4)
-        finish_block(5)
-        second_product(0, 1, 4)
-        place(0, QUARTER, HALF)
-        finish_block(6)
-        finish_block(7)
-        quantise(h_codes[2][:], h_scales[2][:], h_rest[:])
-        second_product(1, 1, 3)
-        place(1, QUARTER, HALF)
-        for m in range(N // P):
-            second_product(m, 2, m)
-            second_product(m, 3, 6 + m)
-        for m in range(N // P):
-            place(m, HALF, S)
-            nc.sync.dma_start(out=out[m * P : (m + 1) * P, :], in_=windows[m][:])
+        prepare_w2(0, tile("w2_rounded0", PACK * P, BF16), nc.scalar.copy)
+        hidden(0)
+        prepare_w2(1, tile_at("w2_rounded1", PACK * P, BF16, 16384), nc.vector.tensor_copy)
+        hidden(1)
+        second_product(0, 0)
+        second_product(1, 0)
+        place(0, 0)
+        hidden(2)
+        second_product(0, 1)
+        second_product(1, 1)
+        place(0, 1)
+        hidden(3)
+        place(1, 0)
+        second_product(0, 2)
+        second_product(1, 2)
+        place(0, 2)
+        place(1, 1)
+        second_product(0, 3)
+        second_product(1, 3)
+        place(0, 3)
+        nc.sync.dma_start(out=out[:P, :], in_=windows[0][:])
+        place(1, 2)
+        place(1, 3)
+        nc.sync.dma_start(out=out[P:, :], in_=windows[1][:])

@@ -26,6 +26,8 @@ BLOCKS = S // BLOCK
 QUARTER = S // 4
 HALF = S // 2
 AHEAD = 6
+FIRST_CUT = 256
+SECOND_CUT = 640
 
 
 def tile_picked_route2_mlprelu_p_kernel(tc, x_words, x_scales, gate, w1, w2, offs, dst, out):
@@ -142,23 +144,21 @@ def tile_picked_route2_mlprelu_p_kernel(tc, x_words, x_scales, gate, w1, w2, off
             for b in range(AHEAD):
                 first_product(0, t, b)
 
-        for lo, hi in ((0, BLOCK), (BLOCK, QUARTER), (QUARTER, HALF), (HALF, S)):
+        for lo, hi in ((0, QUARTER), (QUARTER, HALF), (HALF, S)):
             gather_words1(lo, hi)
 
-        h_codes = [tile("h_codes%d" % c, QUARTER, U32) for c in range(4)]
-        h_scales = [tile("h_scales%d" % c, QUARTER, U8) for c in range(4)]
-        h_rounded = [tile_at("h_rounded0", PACK * QUARTER, BF16, 16384)]
-        h_rounded.extend(tile("h_rounded%d" % c, PACK * QUARTER, BF16) for c in range(1, 4))
+        h_codes = tile("h_codes", S, U32)
+        h_scales = tile("h_scales", S, U8)
 
-        def hidden(c):
-            for b in (2 * c, 2 * c + 1):
+        def hidden(lo, hi, rounded):
+            for b in range(lo // BLOCK, hi // BLOCK):
                 for z in range(1 if b < AHEAD else 0, PASSES):
                     for t in range(PACK):
                         first_product(z, t, b)
-                at = PACK * BLOCK * (b % 2)
-                rounded = h_rounded[c][:, at : at + PACK * BLOCK].rearrange("p (n t) -> p n t", t=PACK)
-                nc.scalar.activation(out=rounded, in_=sums[b][:].rearrange("p (t n) -> p n t", t=PACK), func=RELU)
-            quantise(h_codes[c][:], h_scales[c][:], h_rounded[c][:])
+                at = PACK * (b * BLOCK - lo)
+                block = rounded[:, at : at + PACK * BLOCK].rearrange("p (n t) -> p n t", t=PACK)
+                nc.scalar.activation(out=block, in_=sums[b][:].rearrange("p (t n) -> p n t", t=PACK), func=RELU)
+            quantise(h_codes[:, lo:hi], h_scales[:, lo:hi], rounded[:])
 
         w2_codes = [tile("w2_codes%d" % m, P, U32) for m in range(N // P)]
         w2_scales = [tile("w2_scales%d" % m, P, U8) for m in range(N // P)]
@@ -171,46 +171,39 @@ def tile_picked_route2_mlprelu_p_kernel(tc, x_words, x_scales, gate, w1, w2, off
             quantise(w2_codes[m][:], w2_scales[m][:], rounded[:])
 
         y = [tile("y%d" % m, S, F32) for m in range(N // P)]
-        y_bank = (6, 2, 4, 6)
 
-        def second_product(m, c):
-            cols = slice(c * QUARTER, (c + 1) * QUARTER)
-            product = bank(y_bank[c] + m)
-            multiply(product[:, :QUARTER], w2_codes[m][:], w2_scales[m][:], h_codes[c][:], h_scales[c][:], True, True)
-            if m == 0:
-                nc.scalar.copy(out=y[0][:, cols], in_=product[:, :QUARTER])
-            else:
-                nc.vector.tensor_tensor(y[1][:, cols], product[:, :QUARTER], gate_sb[:, cols], MULT)
+        def second_product(m, lo, hi, bank_number, gated):
+            product = bank(bank_number)[:, : hi - lo]
+            multiply(product, w2_codes[m][:], w2_scales[m][:], h_codes[:, lo:hi], h_scales[:, lo:hi], True, True)
+            if gated > lo:
+                nc.vector.tensor_tensor(y[m][:, lo:gated], product[:, : gated - lo], gate_sb[:, lo:gated], MULT)
+            if gated < hi:
+                nc.scalar.copy(out=y[m][:, gated:hi], in_=product[:, gated - lo :])
 
-        def place(m, c):
-            lo, hi = c * QUARTER, (c + 1) * QUARTER
+        def vector_places(m, lo, hi):
             target = windows[m][:].indirect(entries(dst_sb, lo, hi))
-            if m == 0:
-                nc.vector.tensor_tensor(target, y[0][:, lo:hi], gate_sb[:, lo:hi], MULT)
-            else:
-                nc.scalar.activation(out=target, in_=y[1][:, lo:hi], func=COPY)
+            nc.vector.tensor_tensor(target, y[m][:, lo:hi], gate_sb[:, lo:hi], MULT)
+
+        def scalar_places(lo, hi):
+            nc.scalar.activation(out=windows[1][:].indirect(entries(dst_sb, lo, hi)), in_=y[1][:, lo:hi], func=COPY)
 
         prepare_w2(0, tile("w2_rounded0", PACK * P, BF16), nc.scalar.copy)
-        hidden(0)
+        hidden(0, QUARTER, tile_at("h_first", PACK * QUARTER, BF16, 16384))
         prepare_w2(1, tile_at("w2_rounded1", PACK * P, BF16, 16384), nc.vector.tensor_copy)
-        hidden(1)
-        second_product(0, 0)
-        second_product(1, 0)
-        place(0, 0)
-        hidden(2)
-        second_product(0, 1)
-        second_product(1, 1)
-        place(0, 1)
-        hidden(3)
-        place(1, 0)
-        second_product(0, 2)
-        second_product(1, 2)
-        place(0, 2)
-        place(1, 1)
-        second_product(0, 3)
-        second_product(1, 3)
-        place(0, 3)
+        hidden(QUARTER, HALF, tile("h_second", PACK * QUARTER, BF16))
+        second_product(0, 0, QUARTER, 6, 0)
+        second_product(1, 0, QUARTER, 7, QUARTER)
+        vector_places(0, 0, QUARTER)
+        h_rest = tile("h_rest", PACK * HALF, BF16)
+        hidden(HALF, S, h_rest)
+        second_product(1, QUARTER, HALF, 5, HALF)
+        second_product(0, QUARTER, HALF, 2, QUARTER)
+        vector_places(0, QUARTER, HALF)
+        scalar_places(0, FIRST_CUT)
+        second_product(0, HALF, S, 3, HALF)
+        second_product(1, HALF, S, 4, SECOND_CUT)
+        vector_places(0, HALF, S)
         nc.sync.dma_start(out=out[:P, :], in_=windows[0][:])
-        place(1, 2)
-        place(1, 3)
+        scalar_places(FIRST_CUT, SECOND_CUT)
+        vector_places(1, SECOND_CUT, S)
         nc.sync.dma_start(out=out[P:, :], in_=windows[1][:])

@@ -26,8 +26,8 @@ BLOCKS = S // BLOCK
 QUARTER = S // 4
 HALF = S // 2
 AHEAD = 6
-FIRST_CUT = 256
-SECOND_CUT = 640
+FIRST_CUT = 288
+SECOND_CUT = 672
 
 
 def tile_picked_route2_mlprelu_p_kernel(tc, x_words, x_scales, gate, w1, w2, offs, dst, out):
@@ -65,44 +65,51 @@ def tile_picked_route2_mlprelu_p_kernel(tc, x_words, x_scales, gate, w1, w2, off
 
         offs_sb = tile("offs_sb", S // STRIPE, U16)
         dst_sb = tile("dst_sb", S // STRIPE, U16)
-        scale_rows = tile_at("scale_rows", 3 * T, U8, 7168)[:, :T]
+        scale_rows = tile_at("scale_rows", 3 * T, U8, 15360)[:, :T]
         table0 = tile("table0", T, U32)
-        w1_raw = [tile("w1_raw%d" % z, PACK * H, F32) for z in range(PASSES)]
+        w1_raw = [tile("w1_raw0", PACK * H, F32)]
         windows = [tile("window%d" % m, U, F32) for m in range(N // P)]
         planes = tile("planes", PASSES * S, U8)
-        zero = tile("zero", 16, F32)
+        zeros = [tile_at("zero0", 16, F32, 0), tile("zero1", 16, F32)]
 
         def load_table(table, z):
             nc.sync.dma_start(out=table[:].bitcast(I32), in_=x_words[z].rearrange("p c r -> p (c r)").bitcast(I32))
 
+        def load_w1(z):
+            rows = w1[z * K_PASS : (z + 1) * K_PASS, :]
+            nc.sync.dma_start(out=w1_raw[z][:], in_=rows.rearrange("(p j) c -> p (j c)", j=PACK))
+
         nc.sync.dma_start(out=scale_rows[:32, :].bitcast(I32), in_=x_scales.rearrange("z b c -> b z c").bitcast(I32))
         nc.sync.dma_start(offs_sb[:], offs)
         load_table(table0, 0)
-        for z in range(PASSES):
-            rows = w1[z * K_PASS : (z + 1) * K_PASS, :]
-            nc.sync.dma_start(out=w1_raw[z][:], in_=rows.rearrange("(p j) c -> p (j c)", j=PACK))
+        load_w1(0)
         nc.sync.dma_start(dst_sb[:], dst)
         nc.vector.memset(scale_rows[32:64, :].bitcast(I32), 0)
         nc.vector.memset(scale_rows[64:, :].bitcast(I32), 0)
-        nc.vector.memset(zero[:], 0.0)
+        for zero in zeros:
+            nc.vector.memset(zero[:], 0.0)
         nc.vector.memset(planes[:].bitcast(I32), 0)
-        for window in windows:
+        for window, zero in zip(windows, zeros):
             nc.scalar.copy(out=window[:], in_=zero[:, 0:1].to_broadcast([P, U]))
 
-        picked_rows = tile("picked_rows", S, U8)
-        nc.vector.tensor_copy(picked_rows[:], scale_rows.indirect(offs_sb[:]))
+        def pick_scales(lo, hi, picked):
+            nc.vector.tensor_copy(picked[:], scale_rows.indirect(entries(offs_sb, lo, hi)))
+            for q in range(4):
+                both = planes[32 * q : 32 * q + 4, :].bitcast(I32).rearrange("p (z c) -> p z c", z=PASSES)
+                nc.sync.dma_start(out=both[:, :, lo // 4 : hi // 4], in_=picked[8 * q : 8 * q + 8, :].bitcast(I32))
 
-        for q in range(4):
-            both = planes[32 * q : 32 * q + 4, :].bitcast(I32).rearrange("p (z c) -> p z c", z=PASSES)
-            nc.sync.dma_start(out=both, in_=picked_rows[8 * q : 8 * q + 8, :].bitcast(I32))
+        pick_scales(0, HALF, tile("picked_rows0", HALF, U8))
+        w1_raw.append(tile_at("w1_raw1", PACK * H, F32, 0))
+        load_w1(1)
+        pick_scales(HALF, S, tile("picked_rows1", HALF, U8))
 
-        table1 = tile_at("table1", T, U32, 0)
+        table1 = tile_at("table1", T, U32, 8192)
         load_table(table1, 1)
-        w2_raw = [tile_at("w2_raw%d" % m, PACK * P, F32, 8192 + 2048 * m) for m in range(N // P)]
+        w2_raw = [tile_at("w2_raw%d" % m, PACK * P, F32, 16384 + 2048 * m) for m in range(N // P)]
         for m in range(N // P):
             columns = w2[:, m * P : (m + 1) * P].rearrange("(p t) c -> p t c", t=PACK)
             nc.sync.dma_start(out=w2_raw[m][:].rearrange("p (t c) -> p t c", t=PACK), in_=columns)
-        gate_sb = tile_at("gate_sb", S, F32, 12288)
+        gate_sb = tile_at("gate_sb", S, F32, 20480)
         nc.sync.dma_start(out=gate_sb[:], in_=gate)
 
         words0 = tile("words0", S, U32)
@@ -133,7 +140,7 @@ def tile_picked_route2_mlprelu_p_kernel(tc, x_words, x_scales, gate, w1, w2, off
 
         def first_product(z, t, b):
             if z == 0 and t == 0:
-                sums[b] = bank(b % AHEAD)
+                sums[b] = bank(b if b < AHEAD else b - 3)
             cols = slice(t * P, (t + 1) * P)
             words = words0[:, b * BLOCK : (b + 1) * BLOCK] if z == 0 else words1[b]
             plane = planes[:, z * S + b * BLOCK : z * S + (b + 1) * BLOCK]
@@ -188,8 +195,8 @@ def tile_picked_route2_mlprelu_p_kernel(tc, x_words, x_scales, gate, w1, w2, off
             nc.scalar.activation(out=windows[1][:].indirect(entries(dst_sb, lo, hi)), in_=y[1][:, lo:hi], func=COPY)
 
         prepare_w2(0, tile("w2_rounded0", PACK * P, BF16), nc.scalar.copy)
-        hidden(0, QUARTER, tile_at("h_first", PACK * QUARTER, BF16, 16384))
-        prepare_w2(1, tile_at("w2_rounded1", PACK * P, BF16, 16384), nc.vector.tensor_copy)
+        hidden(0, QUARTER, tile_at("h_first", PACK * QUARTER, BF16, 24576))
+        prepare_w2(1, tile_at("w2_rounded1", PACK * P, BF16, 24576), nc.vector.tensor_copy)
         hidden(QUARTER, HALF, tile("h_second", PACK * QUARTER, BF16))
         second_product(0, 0, QUARTER, 6, 0)
         second_product(1, 0, QUARTER, 7, QUARTER)
@@ -197,11 +204,11 @@ def tile_picked_route2_mlprelu_p_kernel(tc, x_words, x_scales, gate, w1, w2, off
         h_rest = tile("h_rest", PACK * HALF, BF16)
         hidden(HALF, S, h_rest)
         second_product(1, QUARTER, HALF, 5, HALF)
-        second_product(0, QUARTER, HALF, 2, QUARTER)
+        second_product(0, QUARTER, HALF, 3, QUARTER)
         vector_places(0, QUARTER, HALF)
         scalar_places(0, FIRST_CUT)
-        second_product(0, HALF, S, 3, HALF)
-        second_product(1, HALF, S, 4, SECOND_CUT)
+        second_product(0, HALF, S, 1, HALF)
+        second_product(1, HALF, S, 2, SECOND_CUT)
         vector_places(0, HALF, S)
         nc.sync.dma_start(out=out[:P, :], in_=windows[0][:])
         scalar_places(FIRST_CUT, SECOND_CUT)

@@ -26,8 +26,8 @@ BLOCKS = S // BLOCK
 QUARTER = S // 4
 HALF = S // 2
 AHEAD = 6
-FIRST_CUT = 288
-SECOND_CUT = 672
+FIRST_CUT = 320
+SECOND_CUT = 704
 
 
 def tile_picked_route2_mlprelu_p_kernel(tc, x_words, x_scales, gate, w1, w2, offs, dst, out):
@@ -179,13 +179,22 @@ def tile_picked_route2_mlprelu_p_kernel(tc, x_words, x_scales, gate, w1, w2, off
 
         y = [tile("y%d" % m, S, F32) for m in range(N // P)]
 
-        def second_product(m, lo, hi, bank_number, gated):
+        def second_product(m, lo, hi, bank_number):
             product = bank(bank_number)[:, : hi - lo]
-            multiply(product, w2_codes[m][:], w2_scales[m][:], h_codes[:, lo:hi], h_scales[:, lo:hi], True, True)
-            if gated > lo:
-                nc.vector.tensor_tensor(y[m][:, lo:gated], product[:, : gated - lo], gate_sb[:, lo:gated], MULT)
-            if gated < hi:
-                nc.scalar.copy(out=y[m][:, gated:hi], in_=product[:, gated - lo :])
+            at = lo
+            for width in (HALF, QUARTER, BLOCK, BLOCK // 2):
+                if at + width <= hi:
+                    cols = slice(at, at + width)
+                    sums_y = product[:, at - lo : at - lo + width]
+                    multiply(sums_y, w2_codes[m][:], w2_scales[m][:], h_codes[:, cols], h_scales[:, cols], True, True)
+                    at += width
+            return product
+
+        def gated(m, lo, hi, bank_number):
+            nc.vector.tensor_tensor(y[m][:, lo:hi], second_product(m, lo, hi, bank_number), gate_sb[:, lo:hi], MULT)
+
+        def copied(m, lo, hi, bank_number, engine_copy):
+            engine_copy(out=y[m][:, lo:hi], in_=second_product(m, lo, hi, bank_number))
 
         def vector_places(m, lo, hi):
             target = windows[m][:].indirect(entries(dst_sb, lo, hi))
@@ -198,17 +207,17 @@ def tile_picked_route2_mlprelu_p_kernel(tc, x_words, x_scales, gate, w1, w2, off
         hidden(0, QUARTER, tile_at("h_first", PACK * QUARTER, BF16, 24576))
         prepare_w2(1, tile_at("w2_rounded1", PACK * P, BF16, 24576), nc.vector.tensor_copy)
         hidden(QUARTER, HALF, tile("h_second", PACK * QUARTER, BF16))
-        second_product(0, 0, QUARTER, 6, 0)
-        second_product(1, 0, QUARTER, 7, QUARTER)
+        copied(0, 0, QUARTER, 6, nc.scalar.copy)
         vector_places(0, 0, QUARTER)
-        h_rest = tile("h_rest", PACK * HALF, BF16)
-        hidden(HALF, S, h_rest)
-        second_product(1, QUARTER, HALF, 5, HALF)
-        second_product(0, QUARTER, HALF, 3, QUARTER)
+        hidden(HALF, S, tile("h_rest", PACK * HALF, BF16))
+        gated(1, 0, FIRST_CUT, 5)
+        copied(0, QUARTER, HALF, 3, nc.scalar.copy)
         vector_places(0, QUARTER, HALF)
         scalar_places(0, FIRST_CUT)
-        second_product(0, HALF, S, 1, HALF)
-        second_product(1, HALF, S, 2, SECOND_CUT)
+        copied(0, HALF + BLOCK, S, 1, nc.scalar.copy)
+        copied(0, HALF, HALF + BLOCK, 0, nc.vector.tensor_copy)
+        gated(1, FIRST_CUT, SECOND_CUT, 2)
+        copied(1, SECOND_CUT, S, 7, nc.scalar.copy)
         vector_places(0, HALF, S)
         nc.sync.dma_start(out=out[:P, :], in_=windows[0][:])
         scalar_places(FIRST_CUT, SECOND_CUT)

@@ -25,7 +25,7 @@ BLOCK = 128
 BLOCKS = S // BLOCK
 QUARTER = S // 4
 HALF = S // 2
-AHEAD = 6
+AHEAD = 5
 FIRST_CUT = 320
 SECOND_CUT = 704
 
@@ -92,16 +92,20 @@ def tile_picked_route2_mlprelu_p_kernel(tc, x_words, x_scales, gate, w1, w2, off
         for window, zero in zip(windows, zeros):
             nc.scalar.copy(out=window[:], in_=zero[:, 0:1].to_broadcast([P, U]))
 
-        def pick_scales(lo, hi, picked):
+        def pick_scales(lo, hi):
+            picked = tile("picked_rows%d" % lo, hi - lo, U8)
             nc.vector.tensor_copy(picked[:], scale_rows.indirect(entries(offs_sb, lo, hi)))
+            return picked
+
+        def move_scales(lo, hi, picked):
             for q in range(4):
                 both = planes[32 * q : 32 * q + 4, :].bitcast(I32).rearrange("p (z c) -> p z c", z=PASSES)
                 nc.sync.dma_start(out=both[:, :, lo // 4 : hi // 4], in_=picked[8 * q : 8 * q + 8, :].bitcast(I32))
 
-        pick_scales(0, HALF, tile("picked_rows0", HALF, U8))
+        move_scales(0, AHEAD * BLOCK, pick_scales(0, AHEAD * BLOCK))
         w1_raw.append(tile_at("w1_raw1", PACK * H, F32, 0))
         load_w1(1)
-        pick_scales(HALF, S, tile("picked_rows1", HALF, U8))
+        picked_late = pick_scales(AHEAD * BLOCK, S)
 
         table1 = tile_at("table1", T, U32, 8192)
         load_table(table1, 1)
@@ -109,6 +113,7 @@ def tile_picked_route2_mlprelu_p_kernel(tc, x_words, x_scales, gate, w1, w2, off
         for m in range(N // P):
             columns = w2[:, m * P : (m + 1) * P].rearrange("(p t) c -> p t c", t=PACK)
             nc.sync.dma_start(out=w2_raw[m][:].rearrange("p (t c) -> p t c", t=PACK), in_=columns)
+        move_scales(AHEAD * BLOCK, S, picked_late)
         gate_sb = tile_at("gate_sb", S, F32, 20480)
         nc.sync.dma_start(out=gate_sb[:], in_=gate)
 
@@ -140,7 +145,7 @@ def tile_picked_route2_mlprelu_p_kernel(tc, x_words, x_scales, gate, w1, w2, off
 
         def first_product(z, t, b):
             if z == 0 and t == 0:
-                sums[b] = bank(b if b < AHEAD else b - 3)
+                sums[b] = bank(b if b < 6 else b - 3)
             cols = slice(t * P, (t + 1) * P)
             words = words0[:, b * BLOCK : (b + 1) * BLOCK] if z == 0 else words1[b]
             plane = planes[:, z * S + b * BLOCK : z * S + (b + 1) * BLOCK]

@@ -65,11 +65,13 @@ def tile_picked_route2_mlprelu_p_kernel(tc, x_words, x_scales, gate, w1, w2, off
 
         offs_sb = tile("offs_sb", S // STRIPE, U16)
         dst_sb = tile("dst_sb", S // STRIPE, U16)
-        scale_rows = tile_at("scale_rows", 3 * T, U8, 15360)[:, :T]
+        scale_rows = tile_at("scale_rows", 5 * T, U8, 15360)[:, :T]
         table0 = tile("table0", T, U32)
         w1_raw = [tile("w1_raw0", PACK * H, F32)]
         windows = [tile("window%d" % m, U, F32) for m in range(N // P)]
-        planes = tile("planes", PASSES * S, U8)
+        early = AHEAD * BLOCK
+        planes_first = tile("planes_first", early, U8)
+        planes_late = tile("planes_late", PASSES * (S - early), U8)
         zeros = [tile_at("zero0", 16, F32, 0), tile("zero1", 16, F32)]
 
         def load_table(table, z):
@@ -88,7 +90,8 @@ def tile_picked_route2_mlprelu_p_kernel(tc, x_words, x_scales, gate, w1, w2, off
         nc.vector.memset(scale_rows[64:, :].bitcast(I32), 0)
         for zero in zeros:
             nc.vector.memset(zero[:], 0.0)
-        nc.vector.memset(planes[:].bitcast(I32), 0)
+        nc.vector.memset(planes_first[:].bitcast(I32), 0)
+        nc.vector.memset(planes_late[:].bitcast(I32), 0)
         for window, zero in zip(windows, zeros):
             nc.scalar.copy(out=window[:], in_=zero[:, 0:1].to_broadcast([P, U]))
 
@@ -97,25 +100,33 @@ def tile_picked_route2_mlprelu_p_kernel(tc, x_words, x_scales, gate, w1, w2, off
             nc.vector.tensor_copy(picked[:], scale_rows.indirect(entries(offs_sb, lo, hi)))
             return picked
 
-        def move_scales(lo, hi, picked):
-            for q in range(4):
-                both = planes[32 * q : 32 * q + 4, :].bitcast(I32).rearrange("p (z c) -> p z c", z=PASSES)
-                nc.sync.dma_start(out=both[:, :, lo // 4 : hi // 4], in_=picked[8 * q : 8 * q + 8, :].bitcast(I32))
+        def move_scales(planes, picked, first_pass, passes):
+            for q in (0, 2, 1, 3):
+                rows = picked[8 * q + first_pass : 8 * q + 8 : PASSES // passes, :].bitcast(I32)
+                nc.sync.dma_start(out=planes[32 * q : 32 * q + 4, :].bitcast(I32).rearrange("p (z c) -> p z c", z=passes), in_=rows)
 
-        move_scales(0, AHEAD * BLOCK, pick_scales(0, AHEAD * BLOCK))
+        picked_early = pick_scales(0, early)
+        move_scales(planes_first, picked_early, 0, 1)
         w1_raw.append(tile_at("w1_raw1", PACK * H, F32, 0))
         load_w1(1)
-        picked_late = pick_scales(AHEAD * BLOCK, S)
+        picked_late = pick_scales(early, S)
+        planes_second = tile_at("planes_second", early, U8, 24576)
+        nc.vector.memset(planes_second[:].bitcast(I32), 0)
 
         table1 = tile_at("table1", T, U32, 8192)
         load_table(table1, 1)
         w2_raw = [tile_at("w2_raw%d" % m, PACK * P, F32, 16384 + 2048 * m) for m in range(N // P)]
-        for m in range(N // P):
+
+        def load_w2(m):
             columns = w2[:, m * P : (m + 1) * P].rearrange("(p t) c -> p t c", t=PACK)
             nc.sync.dma_start(out=w2_raw[m][:].rearrange("p (t c) -> p t c", t=PACK), in_=columns)
-        move_scales(AHEAD * BLOCK, S, picked_late)
+
+        load_w2(0)
+        move_scales(planes_second, picked_early, 1, 1)
+        load_w2(1)
         gate_sb = tile_at("gate_sb", S, F32, 20480)
         nc.sync.dma_start(out=gate_sb[:], in_=gate)
+        move_scales(planes_late, picked_late, 0, PASSES)
 
         words0 = tile("words0", S, U32)
         nc.vector.tensor_copy(words0[:], table0[:].indirect(offs_sb[:]))
@@ -148,7 +159,11 @@ def tile_picked_route2_mlprelu_p_kernel(tc, x_words, x_scales, gate, w1, w2, off
                 sums[b] = bank(b if b < 6 else b - 3)
             cols = slice(t * P, (t + 1) * P)
             words = words0[:, b * BLOCK : (b + 1) * BLOCK] if z == 0 else words1[b]
-            plane = planes[:, z * S + b * BLOCK : z * S + (b + 1) * BLOCK]
+            if b < AHEAD:
+                plane = (planes_first, planes_second)[z][:, b * BLOCK : (b + 1) * BLOCK]
+            else:
+                at = z * (S - early) + b * BLOCK - early
+                plane = planes_late[:, at : at + BLOCK]
             first, last = (z, t) == (0, 0), (z, t) == (PASSES - 1, PACK - 1)
             multiply(sums[b][:, t * BLOCK : (t + 1) * BLOCK], w1_codes[z][:, cols], w1_scales[z][:, cols], words, plane, first, last)
 
@@ -209,8 +224,8 @@ def tile_picked_route2_mlprelu_p_kernel(tc, x_words, x_scales, gate, w1, w2, off
             nc.scalar.activation(out=windows[1][:].indirect(entries(dst_sb, lo, hi)), in_=y[1][:, lo:hi], func=COPY)
 
         prepare_w2(0, tile("w2_rounded0", PACK * P, BF16), nc.scalar.copy)
-        hidden(0, QUARTER, tile_at("h_first", PACK * QUARTER, BF16, 24576))
-        prepare_w2(1, tile_at("w2_rounded1", PACK * P, BF16, 24576), nc.vector.tensor_copy)
+        hidden(0, QUARTER, tile_at("h_first", PACK * QUARTER, BF16, 26624))
+        prepare_w2(1, tile_at("w2_rounded1", PACK * P, BF16, 26624), nc.vector.tensor_copy)
         hidden(QUARTER, HALF, tile("h_second", PACK * QUARTER, BF16))
         copied(0, 0, QUARTER, 6, nc.scalar.copy)
         vector_places(0, 0, QUARTER)

@@ -101,7 +101,7 @@ def tile_picked_route2_mlprelu_p_kernel(tc, x_words, x_scales, gate, w1, w2, off
             return picked
 
         def move_scales(planes, picked, first_pass, passes):
-            for q in (0, 2, 1, 3):
+            for q in range(4):
                 rows = picked[8 * q + first_pass : 8 * q + 8 : PASSES // passes, :].bitcast(I32)
                 nc.sync.dma_start(out=planes[32 * q : 32 * q + 4, :].bitcast(I32).rearrange("p (z c) -> p z c", z=passes), in_=rows)
 

@@ -38,10 +38,10 @@ def tile_picked_route2_mlprelu_p_kernel(tc, x_words, x_scales, gate, w1, w2, off
         psum = ctx.enter_context(tc.psum_pool(name="psum", bufs=1))
 
         def tile(name, width, dtype):
-            return sb.tile([P, width], dtype, name=name, align_bytes=64)
+            return sb.tile([P, width], dtype, name=name, align_bytes=256)
 
         def tile_at(name, width, dtype, offset):
-            return reused.tile([P, width], dtype, name=name, align_bytes=64, offset=offset)
+            return reused.tile([P, width], dtype, name=name, align_bytes=256, offset=offset)
 
         def bank(number):
             return psum.tile([P, PACK * BLOCK], F32, name="bank%d" % number)

@@ -27,6 +27,7 @@ QUARTER = S // 4
 HALF = S // 2
 AHEAD = 5
 FIRST_CUT = 320
+SCATTER_CUT = 256
 SECOND_CUT = 704
 
 
@@ -90,6 +91,8 @@ def tile_picked_route2_mlprelu_p_kernel(tc, x_words, x_scales, gate, w1, w2, off
         nc.vector.memset(scale_rows[64:, :].bitcast(I32), 0)
         for zero in zeros:
             nc.vector.memset(zero[:], 0.0)
+        one = tile("one", 16, F32)
+        nc.vector.memset(one[:], 1.0)
         nc.vector.memset(planes_first[:].bitcast(I32), 0)
         nc.vector.memset(planes_late[:].bitcast(I32), 0)
         for window, zero in zip(windows, zeros):
@@ -221,7 +224,7 @@ def tile_picked_route2_mlprelu_p_kernel(tc, x_words, x_scales, gate, w1, w2, off
             nc.vector.tensor_tensor(target, y[m][:, lo:hi], gate_sb[:, lo:hi], MULT)
 
         def scalar_places(lo, hi):
-            nc.scalar.activation(out=windows[1][:].indirect(entries(dst_sb, lo, hi)), in_=y[1][:, lo:hi], func=COPY)
+            nc.scalar.activation(out=windows[1][:].indirect(entries(dst_sb, lo, hi)), in_=y[1][:, lo:hi], func=COPY, scale=one[:, 0:1])
 
         prepare_w2(0, tile("w2_rounded0", PACK * P, BF16), nc.scalar.copy)
         hidden(0, QUARTER, tile_at("h_first", PACK * QUARTER, BF16, 26624))
@@ -233,13 +236,12 @@ def tile_picked_route2_mlprelu_p_kernel(tc, x_words, x_scales, gate, w1, w2, off
         gated(1, 0, FIRST_CUT, 5)
         copied(0, QUARTER, HALF, 3, nc.scalar.copy)
         vector_places(0, QUARTER, HALF)
-        scalar_places(0, FIRST_CUT)
-        copied(0, HALF + BLOCK, S, 1, nc.scalar.copy)
-        copied(0, HALF, HALF + BLOCK, 0, nc.vector.tensor_copy)
+        scalar_places(0, SCATTER_CUT)
+        copied(0, HALF, S, 1, nc.scalar.copy)
         gated(1, FIRST_CUT, SECOND_CUT, 2)
         copied(1, SECOND_CUT, S, 7, nc.scalar.copy)
         vector_places(0, HALF, S)
         nc.sync.dma_start(out=out[:P, :], in_=windows[0][:])
-        scalar_places(FIRST_CUT, SECOND_CUT)
+        scalar_places(SCATTER_CUT, SECOND_CUT)
         vector_places(1, SECOND_CUT, S)
         nc.sync.dma_start(out=out[P:, :], in_=windows[1][:])

from contextlib import ExitStack

import concourse.mybir as mybir

K, T, S, H, N, U = 1024, 2048, 1024, 512, 256, 2048
FLOPS = 2 * S * (K * H + H * N)

F32 = mybir.dt.float32
BF16 = mybir.dt.bfloat16
I32 = mybir.dt.int32
U32 = mybir.dt.uint32
U16 = mybir.dt.uint16
U8 = mybir.dt.uint8
FP8X4 = mybir.dt.float8_e4m3fn_x4
RELU = mybir.ActivationFunctionType.Relu
COPY = mybir.ActivationFunctionType.Copy
MULT = mybir.AluOpType.mult

P = 128
PACK = 4
K_PASS = P * PACK
PASSES = K // K_PASS
STRIPE = 16
BLOCK = 128
BLOCKS = S // BLOCK
QUARTER = S // 4
HALF = S // 2
AHEAD = 5
FIRST_CUT = 320
SCATTER_CUT = 256
SECOND_CUT = 704


def tile_picked_route2_mlprelu_p_kernel(tc, x_words, x_scales, gate, w1, w2, offs, dst, out):
    nc = tc.nc
    with ExitStack() as ctx:
        sb = ctx.enter_context(tc.tile_pool(name="sb", bufs=1))
        reused = ctx.enter_context(tc.tile_pool(name="reused", bufs=1))
        psum = ctx.enter_context(tc.psum_pool(name="psum", bufs=1))

        def tile(name, width, dtype):
            return sb.tile([P, width], dtype, name=name, align_bytes=256)

        def tile_at(name, width, dtype, offset):
            return reused.tile([P, width], dtype, name=name, align_bytes=256, offset=offset)

        def bank(number):
            return psum.tile([P, PACK * BLOCK], F32, name="bank%d" % number)

        def entries(list_tile, lo, hi):
            return list_tile[:, lo // STRIPE : hi // STRIPE]

        def quantise(codes, scales, values):
            nc.vector.quantize_mx(out=codes.bitcast(FP8X4), scales=scales, in_=values)

        def multiply(sums, left, left_scales, right, right_scales, start, stop):
            nc.tensor.matmul_mx(
                out=sums,
                lhsT=left.bitcast(FP8X4),
                lhsT_scale=left_scales,
                rhs=right.bitcast(FP8X4),
                rhs_scale=right_scales,
                start=start,
                stop=stop,
            )

        offs_sb = tile("offs_sb", S // STRIPE, U16)
        dst_sb = tile("dst_sb", S // STRIPE, U16)
        scale_rows = tile_at("scale_rows", 5 * T, U8, 15360)[:, :T]
        table0 = tile("table0", T, U32)
        w1_raw = [tile("w1_raw0", PACK * H, F32)]
        windows = [tile("window%d" % m, U, F32) for m in range(N // P)]
        early = AHEAD * BLOCK
        planes_first = tile("planes_first", early, U8)
        planes_late = tile("planes_late", PASSES * (S - early), U8)
        zeros = [tile_at("zero0", 16, F32, 0), tile("zero1", 16, F32)]

        def load_table(table, z):
            nc.sync.dma_start(out=table[:].bitcast(I32), in_=x_words[z].rearrange("p c r -> p (c r)").bitcast(I32))

        def load_w1(z):
            rows = w1[z * K_PASS : (z + 1) * K_PASS, :]
            nc.sync.dma_start(out=w1_raw[z][:], in_=rows.rearrange("(p j) c -> p (j c)", j=PACK))

        nc.sync.dma_start(out=scale_rows[:32, :].bitcast(I32), in_=x_scales.rearrange("z b c -> b z c").bitcast(I32))
        nc.sync.dma_start(offs_sb[:], offs)
        load_table(table0, 0)
        load_w1(0)
        nc.sync.dma_start(dst_sb[:], dst)
        nc.vector.memset(scale_rows[32:64, :].bitcast(I32), 0)
        nc.vector.memset(scale_rows[64:, :].bitcast(I32), 0)
        for zero in zeros:
            nc.vector.memset(zero[:], 0.0)
        one = tile("one", 16, F32)
        nc.vector.memset(one[:], 1.0)
        nc.vector.memset(planes_first[:].bitcast(I32), 0)
        nc.vector.memset(planes_late[:].bitcast(I32), 0)
        for window, zero in zip(windows, zeros):
            nc.scalar.copy(out=window[:], in_=zero[:, 0:1].to_broadcast([P, U]))

        def pick_scales(lo, hi):
            picked = tile("picked_rows%d" % lo, hi - lo, U8)
            nc.vector.tensor_copy(picked[:], scale_rows.indirect(entries(offs_sb, lo, hi)))
            return picked

        def move_scales(planes, picked, first_pass, passes):
            for q in range(4):
                rows = picked[8 * q + first_pass : 8 * q + 8 : PASSES // passes, :].bitcast(I32)
                nc.sync.dma_start(out=planes[32 * q : 32 * q + 4, :].bitcast(I32).rearrange("p (z c) -> p z c", z=passes), in_=rows)

        picked_early = pick_scales(0, early)
        move_scales(planes_first, picked_early, 0, 1)
        w1_raw.append(tile_at("w1_raw1", PACK * H, F32, 0))
        load_w1(1)
        picked_late = pick_scales(early, S)
        planes_second = tile_at("planes_second", early, U8, 24576)
        nc.vector.memset(planes_second[:].bitcast(I32), 0)

        table1 = tile_at("table1", T, U32, 8192)
        load_table(table1, 1)
        w2_raw = [tile_at("w2_raw%d" % m, PACK * P, F32, 16384 + 2048 * m) for m in range(N // P)]

        def load_w2(m):
            columns = w2[:, m * P : (m + 1) * P].rearrange("(p t) c -> p t c", t=PACK)
            nc.sync.dma_start(out=w2_raw[m][:].rearrange("p (t c) -> p t c", t=PACK), in_=columns)

        load_w2(0)
        move_scales(planes_second, picked_early, 1, 1)
        load_w2(1)
        gate_sb = tile_at("gate_sb", S, F32, 20480)
        nc.sync.dma_start(out=gate_sb[:], in_=gate)
        move_scales(planes_late, picked_late, 0, PASSES)

        words0 = tile("words0", S, U32)
        nc.vector.tensor_copy(words0[:], table0[:].indirect(offs_sb[:]))

        w1_codes = [tile("w1_codes%d" % z, H, U32) for z in range(PASSES)]
        w1_scales = [tile("w1_scales%d" % z, H, U8) for z in range(PASSES)]
        for z in range(PASSES):
            rounded = [tile("w1_rounded%d_%d" % (z, u), 2 * K_PASS, BF16) for u in range(2)]
            for u, engine_copy in enumerate((nc.vector.tensor_copy, nc.scalar.copy)):
                engine_copy(
                    out=rounded[u][:].rearrange("p (e m j) -> p m j e", e=2, j=PACK),
                    in_=w1_raw[z][:].rearrange("p (j m u e) -> p u m j e", j=PACK, u=2, e=2)[:, u],
                )
            for u in range(2):
                cols = slice(2 * u * P, (2 * u + 2) * P)
                quantise(w1_codes[z][:, cols], w1_scales[z][:, cols], rounded[u][:])

        words1 = {}

        def gather_words1(lo, hi):
            piece = tile("words1_%d" % lo, hi - lo, U32)
            nc.vector.tensor_copy(piece[:], table1[:].indirect(entries(offs_sb, lo, hi)))
            for at in range(lo, hi, BLOCK):
                words1[at // BLOCK] = piece[:, at - lo : at - lo + BLOCK]

        sums = {}

        def first_product(z, t, b):
            if z == 0 and t == 0:
                sums[b] = bank(b if b < 6 else b - 3)
            cols = slice(t * P, (t + 1) * P)
            words = words0[:, b * BLOCK : (b + 1) * BLOCK] if z == 0 else words1[b]
            if b < AHEAD:
                plane = (planes_first, planes_second)[z][:, b * BLOCK : (b + 1) * BLOCK]
            else:
                at = z * (S - early) + b * BLOCK - early
                plane = planes_late[:, at : at + BLOCK]
            first, last = (z, t) == (0, 0), (z, t) == (PASSES - 1, PACK - 1)
            multiply(sums[b][:, t * BLOCK : (t + 1) * BLOCK], w1_codes[z][:, cols], w1_scales[z][:, cols], words, plane, first, last)

        for t in range(PACK):
            for b in range(AHEAD):
                first_product(0, t, b)

        for lo, hi in ((0, QUARTER), (QUARTER, HALF), (HALF, S)):
            gather_words1(lo, hi)

        h_codes = tile("h_codes", S, U32)
        h_scales = tile("h_scales", S, U8)

        def hidden(lo, hi, rounded):
            for b in range(lo // BLOCK, hi // BLOCK):
                for z in range(1 if b < AHEAD else 0, PASSES):
                    for t in range(PACK):
                        first_product(z, t, b)
                at = PACK * (b * BLOCK - lo)
                block = rounded[:, at : at + PACK * BLOCK].rearrange("p (n t) -> p n t", t=PACK)
                nc.scalar.activation(out=block, in_=sums[b][:].rearrange("p (t n) -> p n t", t=PACK), func=RELU)
            quantise(h_codes[:, lo:hi], h_scales[:, lo:hi], rounded[:])

        w2_codes = [tile("w2_codes%d" % m, P, U32) for m in range(N // P)]
        w2_scales = [tile("w2_scales%d" % m, P, U8) for m in range(N // P)]

        def prepare_w2(m, rounded, engine_copy):
            engine_copy(
                out=rounded[:].rearrange("p (c i t) -> p c t i", i=4, t=PACK),
                in_=w2_raw[m][:].rearrange("p (t c i) -> p c t i", t=PACK, i=4),
            )
            quantise(w2_codes[m][:], w2_scales[m][:], rounded[:])

        y = [tile("y%d" % m, S, F32) for m in range(N // P)]

        def second_product(m, lo, hi, bank_number):
            product = bank(bank_number)[:, : hi - lo]
            at = lo
            for width in (HALF, QUARTER, BLOCK, BLOCK // 2):
                if at + width <= hi:
                    cols = slice(at, at + width)
                    sums_y = product[:, at - lo : at - lo + width]
                    multiply(sums_y, w2_codes[m][:], w2_scales[m][:], h_codes[:, cols], h_scales[:, cols], True, True)
                    at += width
            return product

        def gated(m, lo, hi, bank_number):
            nc.vector.tensor_tensor(y[m][:, lo:hi], second_product(m, lo, hi, bank_number), gate_sb[:, lo:hi], MULT)

        def copied(m, lo, hi, bank_number, engine_copy):
            engine_copy(out=y[m][:, lo:hi], in_=second_product(m, lo, hi, bank_number))

        def vector_places(m, lo, hi):
            target = windows[m][:].indirect(entries(dst_sb, lo, hi))
            nc.vector.tensor_tensor(target, y[m][:, lo:hi], gate_sb[:, lo:hi], MULT)

        def scalar_places(lo, hi):
            nc.scalar.activation(out=windows[1][:].indirect(entries(dst_sb, lo, hi)), in_=y[1][:, lo:hi], func=COPY, scale=one[:, 0:1])

        prepare_w2(0, tile("w2_rounded0", PACK * P, BF16), nc.scalar.copy)
        hidden(0, QUARTER, tile_at("h_first", PACK * QUARTER, BF16, 26624))
        prepare_w2(1, tile_at("w2_rounded1", PACK * P, BF16, 26624), nc.vector.tensor_copy)
        hidden(QUARTER, HALF, tile("h_second", PACK * QUARTER, BF16))
        copied(0, 0, QUARTER, 6, nc.scalar.copy)
        vector_places(0, 0, QUARTER)
        hidden(HALF, S, tile("h_rest", PACK * HALF, BF16))
        gated(1, 0, FIRST_CUT, 5)
        copied(0, QUARTER, HALF, 3, nc.scalar.copy)
        vector_places(0, QUARTER, HALF)
        scalar_places(0, SCATTER_CUT)
        copied(0, HALF, S, 1, nc.scalar.copy)
        gated(1, FIRST_CUT, SECOND_CUT, 2)
        copied(1, SECOND_CUT, S, 7, nc.scalar.copy)
        vector_places(0, HALF, S)
        nc.sync.dma_start(out=out[:P, :], in_=windows[0][:])
        scalar_places(SCATTER_CUT, SECOND_CUT)
        vector_places(1, SECOND_CUT, S)
        nc.sync.dma_start(out=out[P:, :], in_=windows[1][:])
